import numpy as np
import ml_dtypes


def mxq(x, axis, fmt="e4m3"):
    dtype, down = {"e4m3": (ml_dtypes.float8_e4m3fn, 7), "e5m2": (ml_dtypes.float8_e5m2, 14)}[fmt]
    v = np.moveaxis(np.asarray(x, np.float32).astype(ml_dtypes.bfloat16).astype(np.float64), axis, -1)
    blocks = v.reshape(v.shape[:-1] + (-1, 32))
    amax = np.abs(blocks).max(-1, keepdims=True)
    byte = np.maximum(np.where(amax > 0, np.frexp(amax)[1] - 1 + 127, 0) - down, 1)
    scale = np.exp2(byte - 127.0)
    codes = (blocks / scale).astype(np.float32).astype(dtype).astype(np.float64)
    return np.moveaxis((codes * scale).reshape(v.shape), -1, axis)


WIDE = False


def mx_kscale(k):
    if not WIDE:
        return np.ones(k)
    levels = np.array([30, -30])
    if k % 512:
        return np.exp2(np.random.permutation(np.resize(levels, k // 32))).repeat(32)
    a = np.empty((k // 512, 16))
    for p in range(k // 512):
        a[p, :8] = np.random.permutation(np.resize(levels, 8))
        for g in range(8):
            far = levels[np.abs(levels - a[p, g]) >= 10]
            a[p, g + 8] = far[np.random.randint(len(far))]
    return np.exp2(a.ravel()).repeat(32)


BF16 = ml_dtypes.bfloat16


def bf(x):
    return np.asarray(x, np.float32).astype(BF16)


def f64(x):
    return np.asarray(x).astype(np.float64)


E2M1 = np.array([0.0, 0.5, 1.0, 1.5, 2.0, 3.0, 4.0, 6.0, -0.0, -0.5, -1.0, -1.5, -2.0, -3.0, -4.0, -6.0])


def pack_weight(w, fmt):
    k, n = w.shape
    w = f64(bf(w)).reshape(k // 32, 32, n)
    amax = np.abs(w).max(1)
    if fmt == "e4m3":
        byte = np.frexp(amax)[1] - 1 + 127 - 7
    else:
        mant, ex = np.frexp(amax / 6.0)
        byte = np.where(mant > 0.5, ex, ex - 1) + 127
    byte = np.clip(np.where(amax > 0, byte, 1), 1, 254)
    scaled = (w * np.exp2(127.0 - byte)[:, None, :]).reshape(k, n).astype(np.float32)
    by_word = np.ascontiguousarray(scaled.reshape(k // 512, 128, 4, n).transpose(0, 1, 3, 2))
    if fmt == "e4m3":
        words = by_word.astype(ml_dtypes.float8_e4m3fn).view(np.uint8)
    else:
        c = by_word.astype(ml_dtypes.float4_e2m1fn).view(np.uint8) & 0xF
        words = c[..., 0::2] | (c[..., 1::2] << 4)
    return np.ascontiguousarray(words), np.ascontiguousarray(byte.astype(np.uint8).reshape(k // 512, 16, n))


def unpack_weight(words, scales, fmt):
    g, p, n, _ = words.shape
    if fmt == "e4m3":
        vals = np.ascontiguousarray(words).view(ml_dtypes.float8_e4m3fn).astype(np.float64)
    else:
        nib = np.empty((g, p, n, 4), np.uint8)
        nib[..., 0::2] = words & 0xF
        nib[..., 1::2] = words >> 4
        vals = E2M1[nib]
    vals = vals * np.repeat(np.exp2(scales.astype(np.float64) - 127.0), 8, axis=1)[..., None]
    return vals.transpose(0, 1, 3, 2).reshape(g * 512, n)
def pack4(w):
    words, scales = pack_weight(w, "e2m1")
    return words.reshape(words.shape[0], 128, -1), scales


def unpack4(words, scales):
    return unpack_weight(words.reshape(words.shape[0], 128, -1, 2), scales, "e2m1")


A, M, K, N, P = 3, 512, 2048, 1024, 1024


def setup_inputs():
    s, t = mx_kscale(K), mx_kscale(N)
    r = np.linspace(2.0, 80.0, K) + 0.01 * np.random.standard_normal(K)
    qv = np.linspace(4.0, 20.0, N) + 0.01 * np.random.standard_normal(N)
    qm = qv.mean()
    x = r[:, None] * qv
    basis_words, basis_scales = pack4(np.sin(x) / x / s[:, None])
    hist = np.random.standard_normal((A, M, K)) * r * (qm * np.sqrt(2.0 / K)) * s
    form = (1 + 0.1 * np.random.standard_normal((A, N))) / np.sqrt(A) * qv / qm * t
    resp = np.random.standard_normal((N, P)) / np.sqrt(N) / t[:, None]
    return {"hist": bf(hist),
            "basis_words": basis_words,
            "basis_scales": basis_scales,
            "form": bf(form),
            "resp": bf(resp)}


def reference(hist, basis_words, basis_scales, form, resp):
    h = mxq(f64(hist).reshape(A * M, K), 1, "e4m3")
    basis = unpack4(basis_words, basis_scales)
    d = (h @ basis).reshape(A, M, N)
    f = (d * f64(form)[:, None, :]).sum(0)
    return mxq(f, 1, "e5m2") @ mxq(f64(resp), 0, "e4m3")

@@ -1,0 +1,354 @@
+from contextlib import ExitStack
+
+import concourse.mybir as mybir
+from concourse.masks import make_identity
+
+A, M, K, N, L = 3, 512, 2048, 1024, 1024
+FLOPS = 2 * A * M * K * N + 2 * M * N * L
+
+F32 = mybir.dt.float32
+BF16 = mybir.dt.bfloat16
+I32 = mybir.dt.int32
+U32 = mybir.dt.uint32
+U8 = mybir.dt.uint8
+E4M3 = mybir.dt.float8_e4m3fn_x4
+E5M2 = mybir.dt.float8_e5m2_x4
+E2M1 = mybir.dt.float4_e2m1fn_x4
+MULT = mybir.AluOpType.mult
+ADD = mybir.AluOpType.add
+COPY = mybir.ActivationFunctionType.Copy
+
+P = 128
+KP = 512
+G1 = K // KP
+G2 = N // KP
+HALF = M // 2
+TILES = N // P
+GROUPS = [((0, 0), (1, 0)), ((2, 0), (0, 1)), ((1, 1), (2, 1))]
+WARM = 4
+
+
+def tile_powder_pattern_debye_s9_kernel(tc, hist, basis_words, basis_scales, form, resp, out):
+    nc = tc.nc
+    with ExitStack() as ctx:
+        keep = ctx.enter_context(tc.tile_pool(name="keep", bufs=1))
+        stage = ctx.enter_context(tc.tile_pool(name="stage", bufs=3))
+        psum = ctx.enter_context(tc.psum_pool(name="psum", bufs=4))
+        ctx.enter_context(tc.manual_schedule())
+
+        def kept(shape, dtype, name):
+            return keep.tile(shape, dtype, name=name, align_bytes=64)
+
+        warm = kept([P, 512], BF16, "warm")
+        nc.vector.memset(warm[:], 0.0)
+        scales_raw = kept([P, G1 * N], U8, "scales_raw")
+        nc.vector.memset(scales_raw[:].bitcast(I32), 0)
+        form_raw = kept([A * G2, KP], BF16, "form_raw")
+        nc.gpsimd.dma_start(out=form_raw[:], in_=form.rearrange("c (s j) -> (c s) j", s=G2))
+        ident = kept([P, P], F32, "ident")
+        make_identity(nc, ident[:])
+        form_rows = kept([P, KP], BF16, "form_rows")
+        nc.gpsimd.memset(form_rows[:], 0.0)
+        ident_bf = kept([P, P], BF16, "ident_bf")
+        make_identity(nc, ident_bf[:])
+
+        hist_raw = {}
+        basis_raw = []
+
+        def load_hist(grp, part, g0, passes):
+            c, h = GROUPS[grp][part]
+            raw = kept([P, 2, passes * KP], BF16, "hist_%d_%d_%d" % (grp, part, g0))
+            rows = hist[c, h * HALF : (h + 1) * HALF, g0 * KP : (g0 + passes) * KP]
+            nc.sync.dma_start(out=raw[:], in_=rows.rearrange("(i r) k -> r i k", i=2))
+            for g in range(passes):
+                hist_raw[grp, part, g0 + g] = (raw, g)
+
+        def load_basis(g):
+            raw = kept([P, 2 * N], U8, "basis_raw_%d" % g)
+            nc.sync.dma_start(out=raw[:].bitcast(I32), in_=basis_words[g].bitcast(I32))
+            basis_raw.append(raw)
+
+        def load_basis_scales():
+            src = basis_scales.bitcast(I32).rearrange("g (q r) n -> r q g n", r=4)
+            for r in range(4):
+                nc.scalar.dma_start(
+                    out=scales_raw[r:P:32, :].bitcast(I32).rearrange("q (g n) -> q g n", g=G1), in_=src[r]
+                )
+
+        resp_raw = []
+
+        def load_resp(g):
+            raw = kept([P, 4, L], BF16, "resp_raw_%d" % g)
+            src = resp[g * KP : (g + 1) * KP, :].rearrange("(a t b) l -> b a t l", t=4, b=4)
+            for b in range(4):
+                nc.sync.dma_start(out=raw[b:P:4, :, :], in_=src[b])
+            resp_raw.append(raw)
+
+        for g in range(G1):
+            load_hist(0, 0, g, 1)
+            load_hist(0, 1, g, 1)
+            load_basis(g)
+            if g == 0:
+                load_basis_scales()
+        for grp in (1, 2):
+            for g0 in (0, 2):
+                load_hist(grp, 0, g0, 2)
+                load_hist(grp, 1, g0, 2)
+            load_resp(grp - 1)
+
+        basis_codes = {}
+        basis_plane = {}
+
+        def sort_basis(g):
+            codes = kept([P, 2 * N], U8, "basis_codes_%d" % g)
+            nc.vector.tensor_copy(
+                out=codes[:].bitcast(I32).rearrange("p (s t a w) -> p s t a w", s=G2, t=4, w=2),
+                in_=basis_raw[g][:].bitcast(I32).rearrange("p (s a t w) -> p s t a w", s=G2, t=4, w=2),
+            )
+            plane = kept([P, N], U8, "basis_plane_%d" % g)
+            nc.vector.tensor_copy(
+                out=plane[:].bitcast(I32).rearrange("p (s t a) -> p s t a", s=G2, t=4),
+                in_=scales_raw[:, g * N : (g + 1) * N].bitcast(I32).rearrange("p (s a t) -> p s t a", s=G2, t=4),
+            )
+            basis_codes[g] = codes
+            basis_plane[g] = plane
+
+        hist_grouped = {}
+        hist_codes = {}
+        hist_plane = {}
+
+        def turn_hist(grp, g):
+            grouped = stage.tile([P, 4 * KP], BF16, name="hist_grouped", align_bytes=64)
+            hist_grouped[grp, g] = grouped
+            for part in range(2):
+                raw, gl = hist_raw[grp, part, g]
+                bank = psum.tile([P, 2, 2, P], F32, name="turn")
+                for i in range(2):
+                    words = raw[:, i, gl * KP : (gl + 1) * KP].bitcast(F32)
+                    for u in range(2):
+                        nc.tensor.transpose(bank[:, i, u, :], words[:, u : 2 * P : 2], ident[:])
+                dst = grouped[:, part * 2 * KP : (part + 1) * 2 * KP].bitcast(F32)
+                nc.scalar.copy(
+                    out=dst.rearrange("p (i r u) -> p i r u", i=2, u=2),
+                    in_=bank[:].rearrange("p i u r -> p i r u"),
+                )
+
+        def quantize_hist(grp, g):
+            codes = kept([P, KP], U32, "hist_codes_%d_%d" % (grp, g))
+            plane = kept([P, KP], U8, "hist_plane_%d_%d" % (grp, g))
+            nc.vector.quantize_mx(out=codes[:].bitcast(E4M3), scales=plane[:], in_=hist_grouped[grp, g][:])
+            hist_codes[grp, g] = codes
+            hist_plane[grp, g] = plane
+
+        debye_bank = {}
+
+        def debye_pass(grp, j, g):
+            if g == 0:
+                debye_bank[grp, j] = psum.tile([P, 512], F32, name="debye")
+            nc.tensor.matmul_mx(
+                out=debye_bank[grp, j][:],
+                lhsT=basis_codes[g][:, 2 * P * j : 2 * P * (j + 1)].bitcast(E2M1),
+                lhsT_scale=basis_plane[g][:, P * j : P * (j + 1)],
+                rhs=hist_codes[grp, g][:].bitcast(E4M3),
+                rhs_scale=hist_plane[grp, g][:],
+                start=(g == 0),
+                stop=(g == G1 - 1),
+            )
+
+        def debye_tile(grp, j):
+            for g in range(G1):
+                debye_pass(grp, j, g)
+
+        form_cols = kept([P, 4, 8], F32, "form_cols")
+
+        def sort_form():
+            nc.scalar.copy(
+                out=form_rows[: A * G2, :].rearrange("r (t a b) -> r t a b", t=4, b=4),
+                in_=form_raw[:].rearrange("r (a t b) -> r t a b", t=4, b=4),
+            )
+
+        def spread_form():
+            bank = psum.tile([P, 4, 8], F32, name="turn")
+            for t in range(4):
+                nc.tensor.matmul(
+                    bank[:, t, :], lhsT=form_rows[:, t * P : (t + 1) * P], rhs=ident_bf[:, :8], start=True, stop=True
+                )
+            nc.scalar.copy(out=form_cols[:], in_=bank[:])
+
+        partial = {}
+        pattern = {}
+        for h in range(2):
+            for s in range(G2):
+                pattern[h, s] = kept([P, 4, HALF], BF16, "pattern_%d_%d" % (h, s))
+
+        def weigh(grp, j, part):
+            c, h = GROUPS[grp][part]
+            src = debye_bank[grp, j][:, part * HALF : (part + 1) * HALF]
+            row = c * G2 + j // 4
+            col = form_cols[:, j % 4, row : row + 1]
+            if c == 0:
+                partial[h, j] = kept([P, HALF], F32, "partial_%d_%d" % (h, j))
+                nc.scalar.activation(out=partial[h, j][:], in_=src, func=COPY, scale=col)
+            else:
+                dst = partial[h, j][:] if c == 1 else pattern[h, j // 4][:, j % 4, :]
+                nc.vector.scalar_tensor_tensor(
+                    out=dst, in0=src, scalar=col, in1=partial[h, j][:], op0=MULT, op1=ADD
+                )
+
+        def interleave(engine_copy, dst, src):
+            engine_copy(
+                out=dst.rearrange("p (c i t) -> p c t i", i=4, t=4),
+                in_=src.rearrange("p t (c i) -> p c t i", i=4),
+            )
+
+        resp_grouped = {}
+        resp_codes = {}
+        resp_plane = {}
+
+        def group_resp(s, lh):
+            grouped = stage.tile([P, 4 * 512], BF16, name="resp_grouped", align_bytes=64)
+            interleave(nc.vector.tensor_copy, grouped[:], resp_raw[s][:, :, lh * 512 : (lh + 1) * 512])
+            resp_grouped[s, lh] = grouped
+
+        def quantize_resp(s, lh):
+            codes = kept([P, 512], U32, "resp_codes_%d_%d" % (s, lh))
+            plane = kept([P, 512], U8, "resp_plane_%d_%d" % (s, lh))
+            nc.vector.quantize_mx(out=codes[:].bitcast(E4M3), scales=plane[:], in_=resp_grouped[s, lh][:])
+            resp_codes[s, lh] = codes
+            resp_plane[s, lh] = plane
+
+        pattern_grouped = {}
+        pattern_codes = {}
+        pattern_plane = {}
+
+        def group_pattern(h, s, i0, count):
+            grouped = kept([P, 4 * P * count], BF16, "pattern_grouped_%d_%d_%d" % (h, s, i0))
+            interleave(nc.vector.tensor_copy, grouped[:], pattern[h, s][:, :, i0 * P : (i0 + count) * P])
+            pattern_grouped[h, s, i0] = grouped
+
+        def quantize_pattern(h, s, i0, count):
+            codes = kept([P, P * count], U32, "pattern_codes_%d_%d_%d" % (h, s, i0))
+            plane = kept([P, P * count], U8, "pattern_plane_%d_%d_%d" % (h, s, i0))
+            nc.vector.quantize_mx(out=codes[:].bitcast(E5M2), scales=plane[:], in_=pattern_grouped[h, s, i0][:])
+            for i in range(count):
+                pattern_codes[h, s, i0 + i] = codes[:, i * P : (i + 1) * P]
+                pattern_plane[h, s, i0 + i] = plane[:, i * P : (i + 1) * P]
+
+        out_bank = {}
+
+        def response_pass(h, i, lh, s, tag):
+            if s == 0:
+                out_bank[h, i, lh] = psum.tile([P, 512], F32, name=tag)
+            nc.tensor.matmul_mx(
+                out=out_bank[h, i, lh][:],
+                lhsT=pattern_codes[h, s, i].bitcast(E5M2),
+                lhsT_scale=pattern_plane[h, s, i],
+                rhs=resp_codes[s, lh][:].bitcast(E4M3),
+                rhs_scale=resp_plane[s, lh][:],
+                start=(s == 0),
+                stop=(s == G2 - 1),
+            )
+
+        def store(h, i, lh, engine_copy):
+            result = kept([P, 512], F32, "result_%d_%d_%d" % (h, i, lh))
+            engine_copy(out=result[:], in_=out_bank[h, i, lh][:])
+            m0 = h * HALF + i * P
+            nc.sync.dma_start(out=out[m0 : m0 + P, lh * 512 : (lh + 1) * 512], in_=result[:])
+
+        warm_bank = psum.tile([P, 512], F32, name="debye")
+        for w in range(WARM):
+            nc.tensor.matmul(warm_bank[:], lhsT=warm[:, :P], rhs=warm[:], start=True, stop=True)
+
+        turn_hist(0, 0)
+        sort_basis(0)
+        quantize_hist(0, 0)
+        for g in range(1, G1):
+            turn_hist(0, g)
+            sort_basis(g)
+            quantize_hist(0, g)
+            if g == 1:
+                sort_form()
+            for j in range(4):
+                debye_pass(0, j, g - 1)
+        spread_form()
+        turn_hist(1, 0)
+        turn_hist(1, 1)
+        quantize_hist(1, 0)
+        quantize_hist(1, 1)
+        for j in range(4):
+            debye_pass(0, j, G1 - 1)
+            weigh(0, j, 0)
+            weigh(0, j, 1)
+        for j in range(4, TILES):
+            if j == 6:
+                turn_hist(1, 2)
+                turn_hist(1, 3)
+                quantize_hist(1, 2)
+                quantize_hist(1, 3)
+            debye_tile(0, j)
+            weigh(0, j, 0)
+            weigh(0, j, 1)
+            if j == 4:
+                group_resp(0, 0)
+            if j == 6:
+                quantize_resp(0, 0)
+
+        for j in range(TILES):
+            if j in (2, 5):
+                g0 = 0 if j == 2 else 2
+                turn_hist(2, g0)
+                turn_hist(2, g0 + 1)
+            debye_tile(1, j)
+            weigh(1, j, 0)
+            weigh(1, j, 1)
+            if j in (2, 5):
+                quantize_hist(2, g0)
+                quantize_hist(2, g0 + 1)
+            if j == 0:
+                group_resp(0, 1)
+            if j == 1:
+                quantize_resp(0, 1)
+                group_resp(1, 0)
+            if j == 3:
+                quantize_resp(1, 0)
+                group_resp(1, 1)
+            if j == 4:
+                quantize_resp(1, 1)
+                group_pattern(0, 0, 0, 2)
+            if j == 6:
+                quantize_pattern(0, 0, 0, 2)
+
+        for j in range(TILES):
+            debye_tile(2, j)
+            weigh(2, j, 0)
+            if j > 0:
+                weigh(2, j - 1, 1)
+            if j == 0:
+                group_pattern(0, 1, 0, 2)
+            if j == 1:
+                quantize_pattern(0, 1, 0, 2)
+            if j == 2:
+                for lh in range(2):
+                    for s in range(G2):
+                        response_pass(0, 0, lh, s, "turn")
+                    store(0, 0, lh, nc.scalar.copy)
+            if j == 4:
+                group_pattern(1, 0, 0, 2)
+            if j == 5:
+                quantize_pattern(1, 0, 0, 2)
+        weigh(2, TILES - 1, 1)
+        for lh in range(2):
+            for s in range(G2):
+                response_pass(0, 1, lh, s, "debye")
+            store(0, 1, lh, nc.scalar.copy)
+        for i in range(2):
+            for lh in range(2):
+                response_pass(1, i, lh, 0, "turn")
+        for i in range(2):
+            group_pattern(1, 1, i, 1)
+        for i in range(2):
+            quantize_pattern(1, 1, i, 1)
+        for i in range(2):
+            for lh in range(2):
+                response_pass(1, i, lh, 1, "turn")
+                store(1, i, lh, nc.scalar.copy if lh == 0 else nc.vector.tensor_copy)

@@ -25,7 +25,8 @@ G2 = N // KP
 HALF = M // 2
 TILES = N // P
 GROUPS = [((0, 0), (1, 0)), ((2, 0), (0, 1)), ((1, 1), (2, 1))]
-WARM = 4
+EARLY = 1
+STAGGER = 1
 
 
 def tile_powder_pattern_debye_s9_kernel(tc, hist, basis_words, basis_scales, form, resp, out):
@@ -90,11 +91,14 @@ def tile_powder_pattern_debye_s9_kernel(tc, hist, basis_words, basis_scales, for
             load_basis(g)
             if g == 0:
                 load_basis_scales()
-        for grp in (1, 2):
-            for g0 in (0, 2):
-                load_hist(grp, 0, g0, 2)
-                load_hist(grp, 1, g0, 2)
-            load_resp(grp - 1)
+        for g in range(G1):
+            load_hist(1, 0, g, 1)
+            load_hist(1, 1, g, 1)
+        for g0 in (0, 2):
+            load_hist(2, 0, g0, 2)
+            load_hist(2, 1, g0, 2)
+        for s in range(G2):
+            load_resp(s)
 
         basis_codes = {}
         basis_plane = {}
@@ -117,20 +121,41 @@ def tile_powder_pattern_debye_s9_kernel(tc, hist, basis_words, basis_scales, for
         hist_codes = {}
         hist_plane = {}
 
+        hist_sorted = {}
+
+        def sort_hist(grp, g, part, engine_copy):
+            raw, gl = hist_raw[grp, part, g]
+            words = raw[:].bitcast(F32)[:, :, gl * 2 * P : (gl + 1) * 2 * P]
+            ordered = stage.tile([P, 2, 2, P], F32, name="hist_sorted", bufs=8, align_bytes=64)
+            engine_copy(
+                out=ordered[:].rearrange("r i u (c e) -> r i c u e", e=4),
+                in_=words.rearrange("r i (c e u) -> r i c u e", e=4, u=2),
+            )
+            hist_sorted[grp, g, part] = ordered
+
+        turn_bank = {}
+
         def turn_hist(grp, g):
+            for part in range(2):
+                bank = psum.tile([P, 2, 2, P], F32, name="turn")
+                turn_bank[grp, g, part] = bank
+                for i in range(2):
+                    for u in range(2):
+                        if (grp, g, part) in hist_sorted:
+                            src = hist_sorted[grp, g, part][:, i, u, :]
+                        else:
+                            raw, gl = hist_raw[grp, part, g]
+                            src = raw[:, i, gl * KP : (gl + 1) * KP].bitcast(F32)[:, u : 2 * P : 2]
+                        nc.tensor.transpose(bank[:, i, u, :], src, ident[:])
+
+        def group_hist(grp, g):
             grouped = stage.tile([P, 4 * KP], BF16, name="hist_grouped", align_bytes=64)
             hist_grouped[grp, g] = grouped
             for part in range(2):
-                raw, gl = hist_raw[grp, part, g]
-                bank = psum.tile([P, 2, 2, P], F32, name="turn")
-                for i in range(2):
-                    words = raw[:, i, gl * KP : (gl + 1) * KP].bitcast(F32)
-                    for u in range(2):
-                        nc.tensor.transpose(bank[:, i, u, :], words[:, u : 2 * P : 2], ident[:])
                 dst = grouped[:, part * 2 * KP : (part + 1) * 2 * KP].bitcast(F32)
                 nc.scalar.copy(
                     out=dst.rearrange("p (i r u) -> p i r u", i=2, u=2),
-                    in_=bank[:].rearrange("p i u r -> p i r u"),
+                    in_=turn_bank[grp, g, part][:].rearrange("p i u r -> p i r u"),
                 )
 
         def quantize_hist(grp, g):
@@ -181,18 +206,18 @@ def tile_powder_pattern_debye_s9_kernel(tc, hist, basis_words, basis_scales, for
             for s in range(G2):
                 pattern[h, s] = kept([P, 4, HALF], BF16, "pattern_%d_%d" % (h, s))
 
-        def weigh(grp, j, part):
+        def weigh(grp, j, part, lo=0, hi=HALF):
             c, h = GROUPS[grp][part]
-            src = debye_bank[grp, j][:, part * HALF : (part + 1) * HALF]
+            src = debye_bank[grp, j][:, part * HALF + lo : part * HALF + hi]
             row = c * G2 + j // 4
             col = form_cols[:, j % 4, row : row + 1]
             if c == 0:
                 partial[h, j] = kept([P, HALF], F32, "partial_%d_%d" % (h, j))
                 nc.scalar.activation(out=partial[h, j][:], in_=src, func=COPY, scale=col)
             else:
-                dst = partial[h, j][:] if c == 1 else pattern[h, j // 4][:, j % 4, :]
+                dst = partial[h, j][:, lo:hi] if c == 1 else pattern[h, j // 4][:, j % 4, lo:hi]
                 nc.vector.scalar_tensor_tensor(
-                    out=dst, in0=src, scalar=col, in1=partial[h, j][:], op0=MULT, op1=ADD
+                    out=dst, in0=src, scalar=col, in1=partial[h, j][:, lo:hi], op0=MULT, op1=ADD
                 )
 
         def interleave(engine_copy, dst, src):
@@ -205,10 +230,11 @@ def tile_powder_pattern_debye_s9_kernel(tc, hist, basis_words, basis_scales, for
         resp_codes = {}
         resp_plane = {}
 
-        def group_resp(s, lh):
-            grouped = stage.tile([P, 4 * 512], BF16, name="resp_grouped", align_bytes=64)
-            interleave(nc.vector.tensor_copy, grouped[:], resp_raw[s][:, :, lh * 512 : (lh + 1) * 512])
-            resp_grouped[s, lh] = grouped
+        def group_resp(s, lh, engine_copy, lo=0, hi=512):
+            if lo == 0:
+                resp_grouped[s, lh] = stage.tile([P, 4 * 512], BF16, name="resp_grouped", bufs=4, align_bytes=64)
+            src = resp_raw[s][:, :, lh * 512 + lo : lh * 512 + hi]
+            interleave(engine_copy, resp_grouped[s, lh][:, 4 * lo : 4 * hi], src)
 
         def quantize_resp(s, lh):
             codes = kept([P, 512], U32, "resp_codes_%d_%d" % (s, lh))
@@ -221,9 +247,9 @@ def tile_powder_pattern_debye_s9_kernel(tc, hist, basis_words, basis_scales, for
         pattern_codes = {}
         pattern_plane = {}
 
-        def group_pattern(h, s, i0, count):
+        def group_pattern(h, s, i0, count, engine_copy):
             grouped = kept([P, 4 * P * count], BF16, "pattern_grouped_%d_%d_%d" % (h, s, i0))
-            interleave(nc.vector.tensor_copy, grouped[:], pattern[h, s][:, :, i0 * P : (i0 + count) * P])
+            interleave(engine_copy, grouped[:], pattern[h, s][:, :, i0 * P : (i0 + count) * P])
             pattern_grouped[h, s, i0] = grouped
 
         def quantize_pattern(h, s, i0, count):
@@ -255,100 +281,126 @@ def tile_powder_pattern_debye_s9_kernel(tc, hist, basis_words, basis_scales, for
             m0 = h * HALF + i * P
             nc.sync.dma_start(out=out[m0 : m0 + P, lh * 512 : (lh + 1) * 512], in_=result[:])
 
+        V = nc.vector.tensor_copy
+        S = nc.scalar.copy
         warm_bank = psum.tile([P, 512], F32, name="debye")
-        for w in range(WARM):
-            nc.tensor.matmul(warm_bank[:], lhsT=warm[:, :P], rhs=warm[:], start=True, stop=True)
 
+        def warm_up(count):
+            for w in range(count):
+                nc.tensor.matmul(warm_bank[:], lhsT=warm[:, :P], rhs=warm[:], start=True, stop=True)
+
+        def sort_both(grp, g, engine_copy):
+            sort_hist(grp, g, 0, engine_copy)
+            sort_hist(grp, g, 1, engine_copy)
+
+        warm_up(4)
         turn_hist(0, 0)
+        warm_up(2)
         sort_basis(0)
+        group_hist(0, 0)
         quantize_hist(0, 0)
-        for g in range(1, G1):
-            turn_hist(0, g)
-            sort_basis(g)
-            quantize_hist(0, g)
+        for g in range(1, G1 + 1):
+            grp, gg = divmod(g, G1)
+            turn_hist(grp, gg)
+            group_hist(grp, gg)
+            if g < G1:
+                sort_basis(g)
             if g == 1:
                 sort_form()
+            if g == 3:
+                spread_form()
+            sort_both((g + 1) // G1, (g + 1) % G1, V)
+            if g < G1:
+                quantize_hist(grp, gg)
             for j in range(4):
                 debye_pass(0, j, g - 1)
-        spread_form()
-        turn_hist(1, 0)
-        turn_hist(1, 1)
+        sort_both(1, 2, V)
+        weigh(0, 0, 0)
+        weigh(0, 0, 1)
         quantize_hist(1, 0)
-        quantize_hist(1, 1)
-        for j in range(4):
-            debye_pass(0, j, G1 - 1)
+        for j in range(1, 4):
             weigh(0, j, 0)
             weigh(0, j, 1)
         for j in range(4, TILES):
-            if j == 6:
-                turn_hist(1, 2)
-                turn_hist(1, 3)
-                quantize_hist(1, 2)
-                quantize_hist(1, 3)
+            if j < 7:
+                turn_hist(1, j - 3)
+                group_hist(1, j - 3)
             debye_tile(0, j)
+            sort_both((j + 3) // G1, (j + 3) % G1, V)
+            if j < 7:
+                quantize_hist(1, j - 3)
             weigh(0, j, 0)
             weigh(0, j, 1)
-            if j == 4:
-                group_resp(0, 0)
-            if j == 6:
-                quantize_resp(0, 0)
+
+        sort_both(2, 3, S)
 
         for j in range(TILES):
-            if j in (2, 5):
-                g0 = 0 if j == 2 else 2
+            if j in (1, 4):
+                g0 = 0 if j == 1 else 2
                 turn_hist(2, g0)
                 turn_hist(2, g0 + 1)
+                group_hist(2, g0)
+                group_hist(2, g0 + 1)
             debye_tile(1, j)
             weigh(1, j, 0)
             weigh(1, j, 1)
-            if j in (2, 5):
+            if j in (1, 4):
                 quantize_hist(2, g0)
+            if j in (2, 5):
                 quantize_hist(2, g0 + 1)
             if j == 0:
-                group_resp(0, 1)
-            if j == 1:
-                quantize_resp(0, 1)
-                group_resp(1, 0)
+                group_resp(0, 0, V)
+            if j == 2:
+                quantize_resp(0, 0)
+                group_resp(1, 0, S, 0, 256)
             if j == 3:
-                quantize_resp(1, 0)
-                group_resp(1, 1)
-            if j == 4:
-                quantize_resp(1, 1)
-                group_pattern(0, 0, 0, 2)
+                group_resp(0, 1, V)
             if j == 6:
-                quantize_pattern(0, 0, 0, 2)
+                group_pattern(0, 0, 0, 2, V)
+                group_resp(1, 0, S, 256, 512)
+            if j == 7:
+                group_pattern(0, 1, 0, 2, S)
+                group_resp(1, 1, S)
 
+        last = TILES - 1
         for j in range(TILES):
             debye_tile(2, j)
-            weigh(2, j, 0)
+            if j < last:
+                weigh(2, j, 0)
             if j > 0:
                 weigh(2, j - 1, 1)
             if j == 0:
-                group_pattern(0, 1, 0, 2)
+                quantize_pattern(0, 0, 0, 2)
             if j == 1:
-                quantize_pattern(0, 1, 0, 2)
+                quantize_resp(1, 0)
             if j == 2:
-                for lh in range(2):
+                quantize_pattern(0, 1, 0, 2)
+            if j == 3:
+                quantize_resp(0, 1)
+            if j == 4:
+                quantize_resp(1, 1)
+                for lh in range(EARLY):
                     for s in range(G2):
                         response_pass(0, 0, lh, s, "turn")
-                    store(0, 0, lh, nc.scalar.copy)
-            if j == 4:
-                group_pattern(1, 0, 0, 2)
-            if j == 5:
+                    store(0, 0, lh, S)
+                group_pattern(1, 0, 0, 2, S)
+            if j == 6:
                 quantize_pattern(1, 0, 0, 2)
-        weigh(2, TILES - 1, 1)
-        for lh in range(2):
+        for part in range(2):
+            for i in range(2):
+                weigh(2, last, part, i * P, (i + 1) * P)
+        for q in range(EARLY, 4):
             for s in range(G2):
-                response_pass(0, 1, lh, s, "debye")
-            store(0, 1, lh, nc.scalar.copy)
+                response_pass(0, q // 2, q % 2, s, "debye")
+            store(0, q // 2, q % 2, S)
         for i in range(2):
-            for lh in range(2):
-                response_pass(1, i, lh, 0, "turn")
-        for i in range(2):
-            group_pattern(1, 1, i, 1)
+            group_pattern(1, 1, i, 1, V)
         for i in range(2):
             quantize_pattern(1, 1, i, 1)
-        for i in range(2):
+        order = [(0, 0), (0, 1), (1, 0), (1, 1)] if STAGGER else [(0, 0), (1, 0), (0, 1), (1, 1)]
+        for i, s in order:
             for lh in range(2):
-                response_pass(1, i, lh, 1, "turn")
-                store(1, i, lh, nc.scalar.copy if lh == 0 else nc.vector.tensor_copy)
+                response_pass(1, i, lh, s, "turn")
+            if s == 1:
+                for lh in range(2):
+                    store(1, i, lh, S if lh == 0 else V)

@@ -26,7 +26,6 @@ HALF = M // 2
 TILES = N // P
 GROUPS = [((0, 0), (1, 0)), ((2, 0), (0, 1)), ((1, 1), (2, 1))]
 EARLY = 1
-STAGGER = 1
 
 
 def tile_powder_pattern_debye_s9_kernel(tc, hist, basis_words, basis_scales, form, resp, out):
@@ -42,19 +41,21 @@ def tile_powder_pattern_debye_s9_kernel(tc, hist, basis_words, basis_scales, for
 
         warm = kept([P, 512], BF16, "warm")
         nc.vector.memset(warm[:], 0.0)
-        scales_raw = kept([P, G1 * N], U8, "scales_raw")
-        nc.vector.memset(scales_raw[:].bitcast(I32), 0)
-        form_raw = kept([A * G2, KP], BF16, "form_raw")
-        nc.gpsimd.dma_start(out=form_raw[:], in_=form.rearrange("c (s j) -> (c s) j", s=G2))
+        scales_raw = []
+        for s in range(G2):
+            scales_raw.append(kept([P, G1 * KP], U8, "scales_raw_%d" % s))
+            nc.vector.memset(scales_raw[s][:].bitcast(I32), 0)
         ident = kept([P, P], F32, "ident")
         make_identity(nc, ident[:])
+        form_raw = kept([A * G2, KP], BF16, "form_raw")
+        nc.gpsimd.dma_start(out=form_raw[:], in_=form.rearrange("c (s j) -> (c s) j", s=G2))
         form_rows = kept([P, KP], BF16, "form_rows")
-        nc.gpsimd.memset(form_rows[:], 0.0)
-        ident_bf = kept([P, P], BF16, "ident_bf")
-        make_identity(nc, ident_bf[:])
+        nc.vector.memset(form_rows[:], 0.0)
+        ident_bf = kept([P, 8], BF16, "ident_bf")
+        nc.vector.tensor_copy(out=ident_bf[:], in_=ident[:, :8])
 
         hist_raw = {}
-        basis_raw = []
+        basis_raw = {}
 
         def load_hist(grp, part, g0, passes):
             c, h = GROUPS[grp][part]
@@ -64,16 +65,18 @@ def tile_powder_pattern_debye_s9_kernel(tc, hist, basis_words, basis_scales, for
             for g in range(passes):
                 hist_raw[grp, part, g0 + g] = (raw, g)
 
-        def load_basis(g):
-            raw = kept([P, 2 * N], U8, "basis_raw_%d" % g)
-            nc.sync.dma_start(out=raw[:].bitcast(I32), in_=basis_words[g].bitcast(I32))
-            basis_raw.append(raw)
+        def load_basis(s, g0, passes):
+            raw = kept([P, passes, 2 * KP], U8, "basis_raw_%d_%d" % (s, g0))
+            src = basis_words[g0 : g0 + passes, :, s * 2 * KP : (s + 1) * 2 * KP].bitcast(I32)
+            nc.sync.dma_start(out=raw[:].bitcast(I32), in_=src.rearrange("g p w -> p g w"))
+            for g in range(passes):
+                basis_raw[s, g0 + g] = raw[:, g, :]
 
-        def load_basis_scales():
-            src = basis_scales.bitcast(I32).rearrange("g (q r) n -> r q g n", r=4)
+        def load_basis_scales(s, queue):
+            src = basis_scales[:, :, s * KP : (s + 1) * KP].bitcast(I32).rearrange("g (q r) n -> r q g n", r=4)
             for r in range(4):
-                nc.scalar.dma_start(
-                    out=scales_raw[r:P:32, :].bitcast(I32).rearrange("q (g n) -> q g n", g=G1), in_=src[r]
+                queue.dma_start(
+                    out=scales_raw[s][r:P:32, :].bitcast(I32).rearrange("q (g n) -> q g n", g=G1), in_=src[r]
                 )
 
         resp_raw = []
@@ -88,34 +91,40 @@ def tile_powder_pattern_debye_s9_kernel(tc, hist, basis_words, basis_scales, for
         for g in range(G1):
             load_hist(0, 0, g, 1)
             load_hist(0, 1, g, 1)
-            load_basis(g)
+            load_basis(0, g, 1)
             if g == 0:
-                load_basis_scales()
-        for g in range(G1):
-            load_hist(1, 0, g, 1)
-            load_hist(1, 1, g, 1)
-        for g0 in (0, 2):
-            load_hist(2, 0, g0, 2)
-            load_hist(2, 1, g0, 2)
+                load_basis_scales(0, nc.scalar)
+        load_hist(1, 0, 0, 1)
+        load_hist(1, 1, 0, 1)
+        load_basis_scales(1, nc.sync)
+        load_basis(1, 0, G1)
+        load_hist(1, 0, 1, 1)
+        load_hist(1, 1, 1, 1)
+        load_hist(1, 0, 2, 2)
+        load_hist(1, 1, 2, 2)
         for s in range(G2):
             load_resp(s)
+            load_hist(2, 0, 2 * s, 2)
+            load_hist(2, 1, 2 * s, 2)
 
         basis_codes = {}
         basis_plane = {}
 
-        def sort_basis(g):
-            codes = kept([P, 2 * N], U8, "basis_codes_%d" % g)
+        def sort_basis(s, g):
+            codes = kept([P, 2 * KP], U8, "basis_codes_%d_%d" % (g, s))
             nc.vector.tensor_copy(
-                out=codes[:].bitcast(I32).rearrange("p (s t a w) -> p s t a w", s=G2, t=4, w=2),
-                in_=basis_raw[g][:].bitcast(I32).rearrange("p (s a t w) -> p s t a w", s=G2, t=4, w=2),
+                out=codes[:].bitcast(I32).rearrange("p (t a w) -> p t a w", t=4, w=2),
+                in_=basis_raw[s, g].bitcast(I32).rearrange("p (a t w) -> p t a w", t=4, w=2),
             )
-            plane = kept([P, N], U8, "basis_plane_%d" % g)
+            basis_codes[s, g] = codes
+
+        def sort_basis_scales(s):
+            plane = kept([P, G1, KP], U8, "basis_plane_%d" % s)
             nc.vector.tensor_copy(
-                out=plane[:].bitcast(I32).rearrange("p (s t a) -> p s t a", s=G2, t=4),
-                in_=scales_raw[:, g * N : (g + 1) * N].bitcast(I32).rearrange("p (s a t) -> p s t a", s=G2, t=4),
+                out=plane[:].bitcast(I32).rearrange("p g (t a) -> p g t a", t=4),
+                in_=scales_raw[s][:].bitcast(I32).rearrange("p (g a t) -> p g t a", g=G1, t=4),
             )
-            basis_codes[g] = codes
-            basis_plane[g] = plane
+            basis_plane[s] = plane
 
         hist_grouped = {}
         hist_codes = {}
@@ -135,8 +144,8 @@ def tile_powder_pattern_debye_s9_kernel(tc, hist, basis_words, basis_scales, for
 
         turn_bank = {}
 
-        def turn_hist(grp, g):
-            for part in range(2):
+        def turn_hist(grp, g, parts=(0, 1)):
+            for part in parts:
                 bank = psum.tile([P, 2, 2, P], F32, name="turn")
                 turn_bank[grp, g, part] = bank
                 for i in range(2):
@@ -167,22 +176,22 @@ def tile_powder_pattern_debye_s9_kernel(tc, hist, basis_words, basis_scales, for
 
         debye_bank = {}
 
-        def debye_pass(grp, j, g):
+        def debye_pass(grp, j, g, tag="debye"):
             if g == 0:
-                debye_bank[grp, j] = psum.tile([P, 512], F32, name="debye")
+                debye_bank[grp, j] = psum.tile([P, 512], F32, name=tag)
             nc.tensor.matmul_mx(
                 out=debye_bank[grp, j][:],
-                lhsT=basis_codes[g][:, 2 * P * j : 2 * P * (j + 1)].bitcast(E2M1),
-                lhsT_scale=basis_plane[g][:, P * j : P * (j + 1)],
+                lhsT=basis_codes[j // 4, g][:, 2 * P * (j % 4) : 2 * P * (j % 4 + 1)].bitcast(E2M1),
+                lhsT_scale=basis_plane[j // 4][:, g, P * (j % 4) : P * (j % 4 + 1)],
                 rhs=hist_codes[grp, g][:].bitcast(E4M3),
                 rhs_scale=hist_plane[grp, g][:],
                 start=(g == 0),
                 stop=(g == G1 - 1),
             )
 
-        def debye_tile(grp, j):
+        def debye_tile(grp, j, tag="debye"):
             for g in range(G1):
-                debye_pass(grp, j, g)
+                debye_pass(grp, j, g, tag)
 
         form_cols = kept([P, 4, 8], F32, "form_cols")
 
@@ -196,7 +205,7 @@ def tile_powder_pattern_debye_s9_kernel(tc, hist, basis_words, basis_scales, for
             bank = psum.tile([P, 4, 8], F32, name="turn")
             for t in range(4):
                 nc.tensor.matmul(
-                    bank[:, t, :], lhsT=form_rows[:, t * P : (t + 1) * P], rhs=ident_bf[:, :8], start=True, stop=True
+                    bank[:, t, :], lhsT=form_rows[:, t * P : (t + 1) * P], rhs=ident_bf[:], start=True, stop=True
                 )
             nc.scalar.copy(out=form_cols[:], in_=bank[:])
 
@@ -293,10 +302,11 @@ def tile_powder_pattern_debye_s9_kernel(tc, hist, basis_words, basis_scales, for
             sort_hist(grp, g, 0, engine_copy)
             sort_hist(grp, g, 1, engine_copy)
 
-        warm_up(4)
+        warm_up(5)
         turn_hist(0, 0)
-        warm_up(2)
-        sort_basis(0)
+        warm_up(3)
+        sort_basis(0, 0)
+        sort_basis_scales(0)
         group_hist(0, 0)
         quantize_hist(0, 0)
         for g in range(1, G1 + 1):
@@ -304,88 +314,120 @@ def tile_powder_pattern_debye_s9_kernel(tc, hist, basis_words, basis_scales, for
             turn_hist(grp, gg)
             group_hist(grp, gg)
             if g < G1:
-                sort_basis(g)
+                sort_basis(0, g)
             if g == 1:
                 sort_form()
             if g == 3:
                 spread_form()
-            sort_both((g + 1) // G1, (g + 1) % G1, V)
             if g < G1:
+                sort_both((g + 1) // G1, (g + 1) % G1, V)
                 quantize_hist(grp, gg)
             for j in range(4):
                 debye_pass(0, j, g - 1)
-        sort_both(1, 2, V)
+        sort_basis_scales(1)
+        for g in range(G1):
+            sort_basis(1, g)
+        debye_tile(0, 4, "turn")
+        sort_both(1, 1, V)
         weigh(0, 0, 0)
         weigh(0, 0, 1)
         quantize_hist(1, 0)
         for j in range(1, 4):
             weigh(0, j, 0)
             weigh(0, j, 1)
-        for j in range(4, TILES):
-            if j < 7:
-                turn_hist(1, j - 3)
-                group_hist(1, j - 3)
-            debye_tile(0, j)
-            sort_both((j + 3) // G1, (j + 3) % G1, V)
-            if j < 7:
-                quantize_hist(1, j - 3)
-            weigh(0, j, 0)
-            weigh(0, j, 1)
+        debye_tile(0, 5)
+        weigh(0, 4, 0)
+        weigh(0, 4, 1)
+        turn_hist(1, 1)
+        weigh(0, 5, 0)
+        weigh(0, 5, 1)
+        group_hist(1, 1)
+        sort_both(1, 2, V)
+        debye_tile(0, 6)
+        quantize_hist(1, 1)
+        sort_both(1, 3, V)
+        weigh(0, 6, 0)
+        weigh(0, 6, 1)
+        debye_tile(0, 7)
+        weigh(0, 7, 0)
+        weigh(0, 7, 1)
 
-        sort_both(2, 3, S)
-
-        for j in range(TILES):
-            if j in (1, 4):
-                g0 = 0 if j == 1 else 2
-                turn_hist(2, g0)
-                turn_hist(2, g0 + 1)
-                group_hist(2, g0)
-                group_hist(2, g0 + 1)
-            debye_tile(1, j)
+        turn_hist(1, 2)
+        turn_hist(1, 3)
+        group_hist(1, 2)
+        group_hist(1, 3)
+        group_resp(0, 0, V)
+        quantize_hist(1, 2)
+        quantize_hist(1, 3)
+        sort_both(2, 0, S)
+        group_resp(0, 1, V)
+        group_resp(1, 0, S, 0, 256)
+        for g in range(G1):
+            for j in range(4):
+                debye_pass(1, j, g)
+        debye_tile(1, 4, "turn")
+        for j in range(5):
             weigh(1, j, 0)
             weigh(1, j, 1)
-            if j in (1, 4):
-                quantize_hist(2, g0)
-            if j in (2, 5):
-                quantize_hist(2, g0 + 1)
-            if j == 0:
-                group_resp(0, 0, V)
-            if j == 2:
-                quantize_resp(0, 0)
-                group_resp(1, 0, S, 0, 256)
             if j == 3:
-                group_resp(0, 1, V)
-            if j == 6:
-                group_pattern(0, 0, 0, 2, V)
-                group_resp(1, 0, S, 256, 512)
-            if j == 7:
-                group_pattern(0, 1, 0, 2, S)
-                group_resp(1, 1, S)
+                sort_both(2, 1, V)
+        group_resp(1, 0, S, 256, 512)
+        debye_tile(1, 5)
+        turn_hist(2, 0)
+        turn_hist(2, 1)
+        group_pattern(0, 0, 0, 2, V)
+        weigh(1, 5, 0)
+        weigh(1, 5, 1)
+        group_hist(2, 0)
+        group_hist(2, 1)
+        sort_both(2, 2, V)
+        quantize_resp(0, 0)
+        sort_both(2, 3, V)
+        debye_tile(1, 6)
+        quantize_hist(2, 0)
+        weigh(1, 6, 0)
+        weigh(1, 6, 1)
+        quantize_resp(1, 0)
+        debye_tile(1, 7)
+        quantize_hist(2, 1)
+        weigh(1, 7, 1)
+        weigh(1, 7, 0)
 
         last = TILES - 1
-        for j in range(TILES):
+        turn_hist(2, 2)
+        turn_hist(2, 3)
+        group_hist(2, 2)
+        group_hist(2, 3)
+        quantize_resp(0, 1)
+        quantize_hist(2, 2)
+        quantize_pattern(0, 0, 0, 2)
+        quantize_hist(2, 3)
+        group_pattern(0, 1, 0, 2, S)
+        group_resp(1, 1, S)
+        quantize_pattern(0, 1, 0, 2)
+        for g in range(G1):
+            for j in range(4):
+                debye_pass(2, j, g)
+        for lh in range(EARLY):
+            for s in range(G2):
+                response_pass(0, 0, lh, s, "turn")
+        debye_tile(2, 4, "turn")
+        for j in range(5):
+            weigh(2, j, 0)
+            if j > 0:
+                weigh(2, j - 1, 1)
+        for lh in range(EARLY):
+            store(0, 0, lh, S)
+        group_pattern(1, 0, 0, 2, S)
+        quantize_resp(1, 1)
+        weigh(2, 4, 1)
+        for j in range(5, TILES):
             debye_tile(2, j)
             if j < last:
                 weigh(2, j, 0)
-            if j > 0:
-                weigh(2, j - 1, 1)
-            if j == 0:
-                quantize_pattern(0, 0, 0, 2)
-            if j == 1:
-                quantize_resp(1, 0)
-            if j == 2:
-                quantize_pattern(0, 1, 0, 2)
-            if j == 3:
-                quantize_resp(0, 1)
-            if j == 4:
-                quantize_resp(1, 1)
-                for lh in range(EARLY):
-                    for s in range(G2):
-                        response_pass(0, 0, lh, s, "turn")
-                    store(0, 0, lh, S)
-                group_pattern(1, 0, 0, 2, S)
-            if j == 6:
-                quantize_pattern(1, 0, 0, 2)
+                if j == 6:
+                    quantize_pattern(1, 0, 0, 2)
+                weigh(2, j, 1)
         for part in range(2):
             for i in range(2):
                 weigh(2, last, part, i * P, (i + 1) * P)
@@ -397,10 +439,12 @@ def tile_powder_pattern_debye_s9_kernel(tc, hist, basis_words, basis_scales, for
             group_pattern(1, 1, i, 1, V)
         for i in range(2):
             quantize_pattern(1, 1, i, 1)
-        order = [(0, 0), (0, 1), (1, 0), (1, 1)] if STAGGER else [(0, 0), (1, 0), (0, 1), (1, 1)]
-        for i, s in order:
-            for lh in range(2):
-                response_pass(1, i, lh, s, "turn")
-            if s == 1:
-                for lh in range(2):
-                    store(1, i, lh, S if lh == 0 else V)
+        for lh in range(2):
+            response_pass(1, 0, lh, 0, "turn")
+        for lh in range(2):
+            response_pass(1, 0, lh, 1, "turn")
+            store(1, 0, lh, S if lh == 0 else V)
+        for lh in range(2):
+            for s in range(G2):
+                response_pass(1, 1, lh, s, "turn")
+            store(1, 1, lh, S if lh == 0 else V)

@@ -19,13 +19,21 @@ ADD = mybir.AluOpType.add
 COPY = mybir.ActivationFunctionType.Copy
 
 P = 128
-KP = 512
-G1 = K // KP
-G2 = N // KP
+SLOTS = 4
+PASS = P * SLOTS
+BANK = 512
+I_PASSES = K // PASS
+J_PASSES = N // PASS
 HALF = M // 2
-TILES = N // P
+ROW_TILES = HALF // P
+J_TILES = N // P
+FORM_COLS = 8
 GROUPS = [((0, 0), (1, 0)), ((2, 0), (0, 1)), ((1, 1), (2, 1))]
-EARLY = 1
+SUM_TAG, TURN_TAG = "debye", "turn"
+PSUM_BUFS = 4
+OPEN_TILES = PSUM_BUFS
+SORTED_BUFS = 8
+RESP_BUFS = J_PASSES * (L // BANK)
 
 
 def tile_powder_pattern_debye_s9_kernel(tc, hist, basis_words, basis_scales, form, resp, out):
@@ -33,177 +41,175 @@ def tile_powder_pattern_debye_s9_kernel(tc, hist, basis_words, basis_scales, for
     with ExitStack() as ctx:
         keep = ctx.enter_context(tc.tile_pool(name="keep", bufs=1))
         stage = ctx.enter_context(tc.tile_pool(name="stage", bufs=3))
-        psum = ctx.enter_context(tc.psum_pool(name="psum", bufs=4))
+        psum = ctx.enter_context(tc.psum_pool(name="psum", bufs=PSUM_BUFS))
         ctx.enter_context(tc.manual_schedule())
+        on_vector = nc.vector.tensor_copy
+        on_scalar = nc.scalar.copy
 
         def kept(shape, dtype, name):
             return keep.tile(shape, dtype, name=name, align_bytes=64)
 
-        warm = kept([P, 512], BF16, "warm")
-        nc.vector.memset(warm[:], 0.0)
         scales_raw = []
-        for s in range(G2):
-            scales_raw.append(kept([P, G1 * KP], U8, "scales_raw_%d" % s))
+        for s in range(J_PASSES):
+            scales_raw.append(kept([P, I_PASSES * PASS], U8, "scales_raw_%d" % s))
             nc.vector.memset(scales_raw[s][:].bitcast(I32), 0)
         ident = kept([P, P], F32, "ident")
         make_identity(nc, ident[:])
-        form_raw = kept([A * G2, KP], BF16, "form_raw")
-        nc.gpsimd.dma_start(out=form_raw[:], in_=form.rearrange("c (s j) -> (c s) j", s=G2))
-        form_rows = kept([P, KP], BF16, "form_rows")
+        form_raw = kept([A * J_PASSES, PASS], BF16, "form_raw")
+        nc.gpsimd.dma_start(out=form_raw[:], in_=form.rearrange("c (s j) -> (c s) j", s=J_PASSES))
+        form_rows = kept([P, PASS], BF16, "form_rows")
         nc.vector.memset(form_rows[:], 0.0)
-        ident_bf = kept([P, 8], BF16, "ident_bf")
-        nc.vector.tensor_copy(out=ident_bf[:], in_=ident[:, :8])
+        ident_bf = kept([P, FORM_COLS], BF16, "ident_bf")
+        nc.vector.tensor_copy(out=ident_bf[:], in_=ident[:, :FORM_COLS])
 
         hist_raw = {}
         basis_raw = {}
+        resp_raw = []
 
-        def load_hist(grp, part, g0, passes):
-            c, h = GROUPS[grp][part]
-            raw = kept([P, 2, passes * KP], BF16, "hist_%d_%d_%d" % (grp, part, g0))
-            rows = hist[c, h * HALF : (h + 1) * HALF, g0 * KP : (g0 + passes) * KP]
-            nc.sync.dma_start(out=raw[:], in_=rows.rearrange("(i r) k -> r i k", i=2))
-            for g in range(passes):
-                hist_raw[grp, part, g0 + g] = (raw, g)
+        def load_hist(grp, g0, passes):
+            for part, (c, h) in enumerate(GROUPS[grp]):
+                raw = kept([P, ROW_TILES, passes * PASS], BF16, "hist_%d_%d_%d" % (grp, part, g0))
+                rows = hist[c, h * HALF : (h + 1) * HALF, g0 * PASS : (g0 + passes) * PASS]
+                nc.sync.dma_start(out=raw[:], in_=rows.rearrange("(r x) i -> x r i", r=ROW_TILES))
+                for g in range(passes):
+                    hist_raw[grp, part, g0 + g] = (raw, g)
 
         def load_basis(s, g0, passes):
-            raw = kept([P, passes, 2 * KP], U8, "basis_raw_%d_%d" % (s, g0))
-            src = basis_words[g0 : g0 + passes, :, s * 2 * KP : (s + 1) * 2 * KP].bitcast(I32)
+            raw = kept([P, passes, 2 * PASS], U8, "basis_raw_%d_%d" % (s, g0))
+            src = basis_words[g0 : g0 + passes, :, s * 2 * PASS : (s + 1) * 2 * PASS].bitcast(I32)
             nc.sync.dma_start(out=raw[:].bitcast(I32), in_=src.rearrange("g p w -> p g w"))
             for g in range(passes):
                 basis_raw[s, g0 + g] = raw[:, g, :]
 
         def load_basis_scales(s, queue):
-            src = basis_scales[:, :, s * KP : (s + 1) * KP].bitcast(I32).rearrange("g (q r) n -> r q g n", r=4)
-            for r in range(4):
+            src = basis_scales[:, :, s * PASS : (s + 1) * PASS].bitcast(I32).rearrange("g (u v) n -> v u g n", v=4)
+            for v in range(4):
                 queue.dma_start(
-                    out=scales_raw[s][r:P:32, :].bitcast(I32).rearrange("q (g n) -> q g n", g=G1), in_=src[r]
+                    out=scales_raw[s][v:P:32, :].bitcast(I32).rearrange("u (g n) -> u g n", g=I_PASSES), in_=src[v]
                 )
 
-        resp_raw = []
-
-        def load_resp(g):
-            raw = kept([P, 4, L], BF16, "resp_raw_%d" % g)
-            src = resp[g * KP : (g + 1) * KP, :].rearrange("(a t b) l -> b a t l", t=4, b=4)
+        def load_resp(s):
+            raw = kept([P, SLOTS, L], BF16, "resp_raw_%d" % s)
+            src = resp[s * PASS : (s + 1) * PASS, :].rearrange("(a t b) l -> b a t l", t=SLOTS, b=4)
             for b in range(4):
                 nc.sync.dma_start(out=raw[b:P:4, :, :], in_=src[b])
             resp_raw.append(raw)
 
-        for g in range(G1):
-            load_hist(0, 0, g, 1)
-            load_hist(0, 1, g, 1)
+        for g in range(I_PASSES):
+            load_hist(0, g, 1)
             load_basis(0, g, 1)
             if g == 0:
                 load_basis_scales(0, nc.scalar)
-        load_hist(1, 0, 0, 1)
-        load_hist(1, 1, 0, 1)
+        load_hist(1, 0, 1)
         load_basis_scales(1, nc.sync)
-        load_basis(1, 0, G1)
-        load_hist(1, 0, 1, 1)
-        load_hist(1, 1, 1, 1)
-        load_hist(1, 0, 2, 2)
-        load_hist(1, 1, 2, 2)
-        for s in range(G2):
+        load_basis(1, 0, I_PASSES)
+        load_hist(1, 1, 1)
+        load_hist(1, 2, 2)
+        for s in range(J_PASSES):
             load_resp(s)
-            load_hist(2, 0, 2 * s, 2)
-            load_hist(2, 1, 2 * s, 2)
+            load_hist(2, 2 * s, 2)
 
         basis_codes = {}
         basis_plane = {}
 
         def sort_basis(s, g):
-            codes = kept([P, 2 * KP], U8, "basis_codes_%d_%d" % (g, s))
+            codes = kept([P, 2 * PASS], U8, "basis_codes_%d_%d" % (g, s))
             nc.vector.tensor_copy(
-                out=codes[:].bitcast(I32).rearrange("p (t a w) -> p t a w", t=4, w=2),
-                in_=basis_raw[s, g].bitcast(I32).rearrange("p (a t w) -> p t a w", t=4, w=2),
+                out=codes[:].bitcast(I32).rearrange("p (t a w) -> p t a w", t=SLOTS, w=2),
+                in_=basis_raw[s, g].bitcast(I32).rearrange("p (a t w) -> p t a w", t=SLOTS, w=2),
             )
             basis_codes[s, g] = codes
 
         def sort_basis_scales(s):
-            plane = kept([P, G1, KP], U8, "basis_plane_%d" % s)
+            plane = kept([P, I_PASSES, PASS], U8, "basis_plane_%d" % s)
             nc.vector.tensor_copy(
-                out=plane[:].bitcast(I32).rearrange("p g (t a) -> p g t a", t=4),
-                in_=scales_raw[s][:].bitcast(I32).rearrange("p (g a t) -> p g t a", g=G1, t=4),
+                out=plane[:].bitcast(I32).rearrange("p g (t a) -> p g t a", t=SLOTS),
+                in_=scales_raw[s][:].bitcast(I32).rearrange("p (g a t) -> p g t a", g=I_PASSES, t=SLOTS),
             )
             basis_plane[s] = plane
 
+        hist_sorted = {}
+        turn_bank = {}
         hist_grouped = {}
         hist_codes = {}
         hist_plane = {}
 
-        hist_sorted = {}
+        def sort_hist(grp, g, engine_copy):
+            for part in range(2):
+                raw, g_local = hist_raw[grp, part, g]
+                words = raw[:].bitcast(F32)[:, :, g_local * 2 * P : (g_local + 1) * 2 * P]
+                ordered = stage.tile([P, ROW_TILES, 2, P], F32, name="hist_sorted", bufs=SORTED_BUFS, align_bytes=64)
+                engine_copy(
+                    out=ordered[:].rearrange("x r u (y e) -> x r y u e", e=4),
+                    in_=words.rearrange("x r (y e u) -> x r y u e", e=4, u=2),
+                )
+                hist_sorted[grp, g, part] = ordered
 
-        def sort_hist(grp, g, part, engine_copy):
-            raw, gl = hist_raw[grp, part, g]
-            words = raw[:].bitcast(F32)[:, :, gl * 2 * P : (gl + 1) * 2 * P]
-            ordered = stage.tile([P, 2, 2, P], F32, name="hist_sorted", bufs=8, align_bytes=64)
-            engine_copy(
-                out=ordered[:].rearrange("r i u (c e) -> r i c u e", e=4),
-                in_=words.rearrange("r i (c e u) -> r i c u e", e=4, u=2),
-            )
-            hist_sorted[grp, g, part] = ordered
-
-        turn_bank = {}
-
-        def turn_hist(grp, g, parts=(0, 1)):
-            for part in parts:
-                bank = psum.tile([P, 2, 2, P], F32, name="turn")
+        def turn_hist(grp, g):
+            for part in range(2):
+                bank = psum.tile([P, ROW_TILES, 2, P], F32, name=TURN_TAG)
                 turn_bank[grp, g, part] = bank
-                for i in range(2):
+                for r in range(ROW_TILES):
                     for u in range(2):
                         if (grp, g, part) in hist_sorted:
-                            src = hist_sorted[grp, g, part][:, i, u, :]
+                            src = hist_sorted[grp, g, part][:, r, u, :]
                         else:
-                            raw, gl = hist_raw[grp, part, g]
-                            src = raw[:, i, gl * KP : (gl + 1) * KP].bitcast(F32)[:, u : 2 * P : 2]
-                        nc.tensor.transpose(bank[:, i, u, :], src, ident[:])
+                            raw, g_local = hist_raw[grp, part, g]
+                            src = raw[:, r, g_local * PASS : (g_local + 1) * PASS].bitcast(F32)[:, u : 2 * P : 2]
+                        nc.tensor.transpose(bank[:, r, u, :], src, ident[:])
 
         def group_hist(grp, g):
-            grouped = stage.tile([P, 4 * KP], BF16, name="hist_grouped", align_bytes=64)
+            grouped = stage.tile([P, SLOTS * BANK], BF16, name="hist_grouped", align_bytes=64)
             hist_grouped[grp, g] = grouped
             for part in range(2):
-                dst = grouped[:, part * 2 * KP : (part + 1) * 2 * KP].bitcast(F32)
+                dst = grouped[:, part * SLOTS * HALF : (part + 1) * SLOTS * HALF].bitcast(F32)
                 nc.scalar.copy(
-                    out=dst.rearrange("p (i r u) -> p i r u", i=2, u=2),
-                    in_=turn_bank[grp, g, part][:].rearrange("p i u r -> p i r u"),
+                    out=dst.rearrange("p (r x u) -> p r x u", r=ROW_TILES, u=2),
+                    in_=turn_bank[grp, g, part][:].rearrange("p r u x -> p r x u"),
                 )
 
         def quantize_hist(grp, g):
-            codes = kept([P, KP], U32, "hist_codes_%d_%d" % (grp, g))
-            plane = kept([P, KP], U8, "hist_plane_%d_%d" % (grp, g))
+            codes = kept([P, BANK], U32, "hist_codes_%d_%d" % (grp, g))
+            plane = kept([P, BANK], U8, "hist_plane_%d_%d" % (grp, g))
             nc.vector.quantize_mx(out=codes[:].bitcast(E4M3), scales=plane[:], in_=hist_grouped[grp, g][:])
             hist_codes[grp, g] = codes
             hist_plane[grp, g] = plane
 
         debye_bank = {}
 
-        def debye_pass(grp, j, g, tag="debye"):
+        def debye_pass(grp, tile, g, tag=SUM_TAG):
+            s, t = divmod(tile, SLOTS)
             if g == 0:
-                debye_bank[grp, j] = psum.tile([P, 512], F32, name=tag)
+                debye_bank[grp, tile] = psum.tile([P, BANK], F32, name=tag)
             nc.tensor.matmul_mx(
-                out=debye_bank[grp, j][:],
-                lhsT=basis_codes[j // 4, g][:, 2 * P * (j % 4) : 2 * P * (j % 4 + 1)].bitcast(E2M1),
-                lhsT_scale=basis_plane[j // 4][:, g, P * (j % 4) : P * (j % 4 + 1)],
+                out=debye_bank[grp, tile][:],
+                lhsT=basis_codes[s, g][:, 2 * P * t : 2 * P * (t + 1)].bitcast(E2M1),
+                lhsT_scale=basis_plane[s][:, g, P * t : P * (t + 1)],
                 rhs=hist_codes[grp, g][:].bitcast(E4M3),
                 rhs_scale=hist_plane[grp, g][:],
                 start=(g == 0),
-                stop=(g == G1 - 1),
+                stop=(g == I_PASSES - 1),
             )
 
-        def debye_tile(grp, j, tag="debye"):
-            for g in range(G1):
-                debye_pass(grp, j, g, tag)
+        def debye_step(grp, g):
+            for tile in range(OPEN_TILES):
+                debye_pass(grp, tile, g)
 
-        form_cols = kept([P, 4, 8], F32, "form_cols")
+        def debye_tile(grp, tile, tag=SUM_TAG):
+            for g in range(I_PASSES):
+                debye_pass(grp, tile, g, tag)
+
+        form_cols = kept([P, SLOTS, FORM_COLS], F32, "form_cols")
 
         def sort_form():
             nc.scalar.copy(
-                out=form_rows[: A * G2, :].rearrange("r (t a b) -> r t a b", t=4, b=4),
-                in_=form_raw[:].rearrange("r (a t b) -> r t a b", t=4, b=4),
+                out=form_rows[: A * J_PASSES, :].rearrange("n (t a b) -> n t a b", t=SLOTS, b=4),
+                in_=form_raw[:].rearrange("n (a t b) -> n t a b", t=SLOTS, b=4),
             )
 
         def spread_form():
-            bank = psum.tile([P, 4, 8], F32, name="turn")
-            for t in range(4):
+            bank = psum.tile([P, SLOTS, FORM_COLS], F32, name=TURN_TAG)
+            for t in range(SLOTS):
                 nc.tensor.matmul(
                     bank[:, t, :], lhsT=form_rows[:, t * P : (t + 1) * P], rhs=ident_bf[:], start=True, stop=True
                 )
@@ -212,42 +218,49 @@ def tile_powder_pattern_debye_s9_kernel(tc, hist, basis_words, basis_scales, for
         partial = {}
         pattern = {}
         for h in range(2):
-            for s in range(G2):
-                pattern[h, s] = kept([P, 4, HALF], BF16, "pattern_%d_%d" % (h, s))
+            for s in range(J_PASSES):
+                pattern[h, s] = kept([P, SLOTS, HALF], BF16, "pattern_%d_%d" % (h, s))
 
-        def weigh(grp, j, part, lo=0, hi=HALF):
+        def weigh(grp, tile, part, lo=0, hi=HALF):
             c, h = GROUPS[grp][part]
-            src = debye_bank[grp, j][:, part * HALF + lo : part * HALF + hi]
-            row = c * G2 + j // 4
-            col = form_cols[:, j % 4, row : row + 1]
+            s, t = divmod(tile, SLOTS)
+            src = debye_bank[grp, tile][:, part * HALF + lo : part * HALF + hi]
+            row = c * J_PASSES + s
+            weight = form_cols[:, t, row : row + 1]
             if c == 0:
-                partial[h, j] = kept([P, HALF], F32, "partial_%d_%d" % (h, j))
-                nc.scalar.activation(out=partial[h, j][:], in_=src, func=COPY, scale=col)
+                partial[h, tile] = kept([P, HALF], F32, "partial_%d_%d" % (h, tile))
+                nc.scalar.activation(out=partial[h, tile][:], in_=src, func=COPY, scale=weight)
             else:
-                dst = partial[h, j][:, lo:hi] if c == 1 else pattern[h, j // 4][:, j % 4, lo:hi]
+                dst = pattern[h, s][:, t, lo:hi] if c == A - 1 else partial[h, tile][:, lo:hi]
                 nc.vector.scalar_tensor_tensor(
-                    out=dst, in0=src, scalar=col, in1=partial[h, j][:, lo:hi], op0=MULT, op1=ADD
+                    out=dst, in0=src, scalar=weight, in1=partial[h, tile][:, lo:hi], op0=MULT, op1=ADD
                 )
+
+        def weigh_both(grp, tile):
+            weigh(grp, tile, 0)
+            weigh(grp, tile, 1)
 
         def interleave(engine_copy, dst, src):
             engine_copy(
-                out=dst.rearrange("p (c i t) -> p c t i", i=4, t=4),
-                in_=src.rearrange("p t (c i) -> p c t i", i=4),
+                out=dst.rearrange("p (y e t) -> p y t e", e=4, t=SLOTS),
+                in_=src.rearrange("p t (y e) -> p y t e", e=4),
             )
 
         resp_grouped = {}
         resp_codes = {}
         resp_plane = {}
 
-        def group_resp(s, lh, engine_copy, lo=0, hi=512):
+        def group_resp(s, lh, engine_copy, lo=0, hi=BANK):
             if lo == 0:
-                resp_grouped[s, lh] = stage.tile([P, 4 * 512], BF16, name="resp_grouped", bufs=4, align_bytes=64)
-            src = resp_raw[s][:, :, lh * 512 + lo : lh * 512 + hi]
-            interleave(engine_copy, resp_grouped[s, lh][:, 4 * lo : 4 * hi], src)
+                resp_grouped[s, lh] = stage.tile(
+                    [P, SLOTS * BANK], BF16, name="resp_grouped", bufs=RESP_BUFS, align_bytes=64
+                )
+            src = resp_raw[s][:, :, lh * BANK + lo : lh * BANK + hi]
+            interleave(engine_copy, resp_grouped[s, lh][:, SLOTS * lo : SLOTS * hi], src)
 
         def quantize_resp(s, lh):
-            codes = kept([P, 512], U32, "resp_codes_%d_%d" % (s, lh))
-            plane = kept([P, 512], U8, "resp_plane_%d_%d" % (s, lh))
+            codes = kept([P, BANK], U32, "resp_codes_%d_%d" % (s, lh))
+            plane = kept([P, BANK], U8, "resp_plane_%d_%d" % (s, lh))
             nc.vector.quantize_mx(out=codes[:].bitcast(E4M3), scales=plane[:], in_=resp_grouped[s, lh][:])
             resp_codes[s, lh] = codes
             resp_plane[s, lh] = plane
@@ -256,195 +269,170 @@ def tile_powder_pattern_debye_s9_kernel(tc, hist, basis_words, basis_scales, for
         pattern_codes = {}
         pattern_plane = {}
 
-        def group_pattern(h, s, i0, count, engine_copy):
-            grouped = kept([P, 4 * P * count], BF16, "pattern_grouped_%d_%d_%d" % (h, s, i0))
-            interleave(engine_copy, grouped[:], pattern[h, s][:, :, i0 * P : (i0 + count) * P])
-            pattern_grouped[h, s, i0] = grouped
+        def group_pattern(h, s, engine_copy, r0=0, count=ROW_TILES):
+            grouped = kept([P, SLOTS * P * count], BF16, "pattern_grouped_%d_%d_%d" % (h, s, r0))
+            interleave(engine_copy, grouped[:], pattern[h, s][:, :, r0 * P : (r0 + count) * P])
+            pattern_grouped[h, s, r0] = grouped
 
-        def quantize_pattern(h, s, i0, count):
-            codes = kept([P, P * count], U32, "pattern_codes_%d_%d_%d" % (h, s, i0))
-            plane = kept([P, P * count], U8, "pattern_plane_%d_%d_%d" % (h, s, i0))
-            nc.vector.quantize_mx(out=codes[:].bitcast(E5M2), scales=plane[:], in_=pattern_grouped[h, s, i0][:])
-            for i in range(count):
-                pattern_codes[h, s, i0 + i] = codes[:, i * P : (i + 1) * P]
-                pattern_plane[h, s, i0 + i] = plane[:, i * P : (i + 1) * P]
+        def quantize_pattern(h, s, r0=0, count=ROW_TILES):
+            codes = kept([P, P * count], U32, "pattern_codes_%d_%d_%d" % (h, s, r0))
+            plane = kept([P, P * count], U8, "pattern_plane_%d_%d_%d" % (h, s, r0))
+            nc.vector.quantize_mx(out=codes[:].bitcast(E5M2), scales=plane[:], in_=pattern_grouped[h, s, r0][:])
+            for r in range(count):
+                pattern_codes[h, s, r0 + r] = codes[:, r * P : (r + 1) * P]
+                pattern_plane[h, s, r0 + r] = plane[:, r * P : (r + 1) * P]
 
         out_bank = {}
 
-        def response_pass(h, i, lh, s, tag):
+        def response_pass(h, r, lh, s, tag):
             if s == 0:
-                out_bank[h, i, lh] = psum.tile([P, 512], F32, name=tag)
+                out_bank[h, r, lh] = psum.tile([P, BANK], F32, name=tag)
             nc.tensor.matmul_mx(
-                out=out_bank[h, i, lh][:],
-                lhsT=pattern_codes[h, s, i].bitcast(E5M2),
-                lhsT_scale=pattern_plane[h, s, i],
+                out=out_bank[h, r, lh][:],
+                lhsT=pattern_codes[h, s, r].bitcast(E5M2),
+                lhsT_scale=pattern_plane[h, s, r],
                 rhs=resp_codes[s, lh][:].bitcast(E4M3),
                 rhs_scale=resp_plane[s, lh][:],
                 start=(s == 0),
-                stop=(s == G2 - 1),
+                stop=(s == J_PASSES - 1),
             )
 
-        def store(h, i, lh, engine_copy):
-            result = kept([P, 512], F32, "result_%d_%d_%d" % (h, i, lh))
-            engine_copy(out=result[:], in_=out_bank[h, i, lh][:])
-            m0 = h * HALF + i * P
-            nc.sync.dma_start(out=out[m0 : m0 + P, lh * 512 : (lh + 1) * 512], in_=result[:])
+        def response_tile(h, r, lh, tag):
+            for s in range(J_PASSES):
+                response_pass(h, r, lh, s, tag)
 
-        V = nc.vector.tensor_copy
-        S = nc.scalar.copy
-        warm_bank = psum.tile([P, 512], F32, name="debye")
+        def store(h, r, lh, engine_copy):
+            result = kept([P, BANK], F32, "result_%d_%d_%d" % (h, r, lh))
+            engine_copy(out=result[:], in_=out_bank[h, r, lh][:])
+            m0 = h * HALF + r * P
+            nc.sync.dma_start(out=out[m0 : m0 + P, lh * BANK : (lh + 1) * BANK], in_=result[:])
 
-        def warm_up(count):
-            for w in range(count):
-                nc.tensor.matmul(warm_bank[:], lhsT=warm[:, :P], rhs=warm[:], start=True, stop=True)
-
-        def sort_both(grp, g, engine_copy):
-            sort_hist(grp, g, 0, engine_copy)
-            sort_hist(grp, g, 1, engine_copy)
-
-        warm_up(5)
         turn_hist(0, 0)
-        warm_up(3)
         sort_basis(0, 0)
         sort_basis_scales(0)
         group_hist(0, 0)
         quantize_hist(0, 0)
-        for g in range(1, G1 + 1):
-            grp, gg = divmod(g, G1)
-            turn_hist(grp, gg)
-            group_hist(grp, gg)
-            if g < G1:
-                sort_basis(0, g)
+        for g in range(1, I_PASSES):
+            turn_hist(0, g)
+            group_hist(0, g)
+            sort_basis(0, g)
             if g == 1:
                 sort_form()
-            if g == 3:
+            if g == I_PASSES - 1:
                 spread_form()
-            if g < G1:
-                sort_both((g + 1) // G1, (g + 1) % G1, V)
-                quantize_hist(grp, gg)
-            for j in range(4):
-                debye_pass(0, j, g - 1)
+            ahead_grp, ahead_g = divmod(g + 1, I_PASSES)
+            sort_hist(ahead_grp, ahead_g, on_vector)
+            quantize_hist(0, g)
+            debye_step(0, g - 1)
+        turn_hist(1, 0)
+        group_hist(1, 0)
+        debye_step(0, I_PASSES - 1)
         sort_basis_scales(1)
-        for g in range(G1):
+        for g in range(I_PASSES):
             sort_basis(1, g)
-        debye_tile(0, 4, "turn")
-        sort_both(1, 1, V)
-        weigh(0, 0, 0)
-        weigh(0, 0, 1)
+        debye_tile(0, 4, TURN_TAG)
+        sort_hist(1, 1, on_vector)
+        weigh_both(0, 0)
         quantize_hist(1, 0)
-        for j in range(1, 4):
-            weigh(0, j, 0)
-            weigh(0, j, 1)
+        for tile in range(1, OPEN_TILES):
+            weigh_both(0, tile)
         debye_tile(0, 5)
-        weigh(0, 4, 0)
-        weigh(0, 4, 1)
+        weigh_both(0, 4)
         turn_hist(1, 1)
-        weigh(0, 5, 0)
-        weigh(0, 5, 1)
+        weigh_both(0, 5)
         group_hist(1, 1)
-        sort_both(1, 2, V)
+        sort_hist(1, 2, on_vector)
         debye_tile(0, 6)
         quantize_hist(1, 1)
-        sort_both(1, 3, V)
-        weigh(0, 6, 0)
-        weigh(0, 6, 1)
+        sort_hist(1, 3, on_vector)
+        weigh_both(0, 6)
         debye_tile(0, 7)
-        weigh(0, 7, 0)
-        weigh(0, 7, 1)
+        weigh_both(0, 7)
 
-        turn_hist(1, 2)
-        turn_hist(1, 3)
-        group_hist(1, 2)
-        group_hist(1, 3)
-        group_resp(0, 0, V)
-        quantize_hist(1, 2)
-        quantize_hist(1, 3)
-        sort_both(2, 0, S)
-        group_resp(0, 1, V)
-        group_resp(1, 0, S, 0, 256)
-        for g in range(G1):
-            for j in range(4):
-                debye_pass(1, j, g)
-        debye_tile(1, 4, "turn")
-        for j in range(5):
-            weigh(1, j, 0)
-            weigh(1, j, 1)
-            if j == 3:
-                sort_both(2, 1, V)
-        group_resp(1, 0, S, 256, 512)
+        for g in (2, 3):
+            turn_hist(1, g)
+        for g in (2, 3):
+            group_hist(1, g)
+        group_resp(0, 0, on_vector)
+        for g in (2, 3):
+            quantize_hist(1, g)
+        sort_hist(2, 0, on_scalar)
+        group_resp(0, 1, on_vector)
+        group_resp(1, 0, on_scalar, 0, BANK // 2)
+        for g in range(I_PASSES):
+            debye_step(1, g)
+        debye_tile(1, 4, TURN_TAG)
+        for tile in range(OPEN_TILES):
+            weigh_both(1, tile)
+        sort_hist(2, 1, on_vector)
+        weigh_both(1, 4)
+        group_resp(1, 0, on_scalar, BANK // 2, BANK)
         debye_tile(1, 5)
-        turn_hist(2, 0)
-        turn_hist(2, 1)
-        group_pattern(0, 0, 0, 2, V)
-        weigh(1, 5, 0)
-        weigh(1, 5, 1)
-        group_hist(2, 0)
-        group_hist(2, 1)
-        sort_both(2, 2, V)
+        for g in (0, 1):
+            turn_hist(2, g)
+        group_pattern(0, 0, on_vector)
+        weigh_both(1, 5)
+        for g in (0, 1):
+            group_hist(2, g)
+        sort_hist(2, 2, on_vector)
         quantize_resp(0, 0)
-        sort_both(2, 3, V)
+        sort_hist(2, 3, on_vector)
         debye_tile(1, 6)
         quantize_hist(2, 0)
-        weigh(1, 6, 0)
-        weigh(1, 6, 1)
+        weigh_both(1, 6)
         quantize_resp(1, 0)
         debye_tile(1, 7)
         quantize_hist(2, 1)
         weigh(1, 7, 1)
         weigh(1, 7, 0)
 
-        last = TILES - 1
-        turn_hist(2, 2)
-        turn_hist(2, 3)
-        group_hist(2, 2)
-        group_hist(2, 3)
+        for g in (2, 3):
+            turn_hist(2, g)
+        for g in (2, 3):
+            group_hist(2, g)
         quantize_resp(0, 1)
         quantize_hist(2, 2)
-        quantize_pattern(0, 0, 0, 2)
+        quantize_pattern(0, 0)
         quantize_hist(2, 3)
-        group_pattern(0, 1, 0, 2, S)
-        group_resp(1, 1, S)
-        quantize_pattern(0, 1, 0, 2)
-        for g in range(G1):
-            for j in range(4):
-                debye_pass(2, j, g)
-        for lh in range(EARLY):
-            for s in range(G2):
-                response_pass(0, 0, lh, s, "turn")
-        debye_tile(2, 4, "turn")
-        for j in range(5):
-            weigh(2, j, 0)
-            if j > 0:
-                weigh(2, j - 1, 1)
-        for lh in range(EARLY):
-            store(0, 0, lh, S)
-        group_pattern(1, 0, 0, 2, S)
+        group_pattern(0, 1, on_scalar)
+        group_resp(1, 1, on_scalar)
+        quantize_pattern(0, 1)
+        for g in range(I_PASSES):
+            debye_step(2, g)
+        response_tile(0, 0, 0, TURN_TAG)
+        debye_tile(2, 4, TURN_TAG)
+        weigh(2, 0, 0)
+        for tile in range(1, OPEN_TILES + 1):
+            weigh(2, tile, 0)
+            weigh(2, tile - 1, 1)
+        store(0, 0, 0, on_scalar)
+        group_pattern(1, 0, on_scalar)
         quantize_resp(1, 1)
         weigh(2, 4, 1)
-        for j in range(5, TILES):
-            debye_tile(2, j)
-            if j < last:
-                weigh(2, j, 0)
-                if j == 6:
-                    quantize_pattern(1, 0, 0, 2)
-                weigh(2, j, 1)
+        debye_tile(2, 5)
+        weigh_both(2, 5)
+        debye_tile(2, 6)
+        weigh(2, 6, 0)
+        quantize_pattern(1, 0)
+        weigh(2, 6, 1)
+        debye_tile(2, 7)
+
         for part in range(2):
-            for i in range(2):
-                weigh(2, last, part, i * P, (i + 1) * P)
-        for q in range(EARLY, 4):
-            for s in range(G2):
-                response_pass(0, q // 2, q % 2, s, "debye")
-            store(0, q // 2, q % 2, S)
-        for i in range(2):
-            group_pattern(1, 1, i, 1, V)
-        for i in range(2):
-            quantize_pattern(1, 1, i, 1)
+            for r in range(ROW_TILES):
+                weigh(2, J_TILES - 1, part, r * P, (r + 1) * P)
+        for r, lh in ((0, 1), (1, 0), (1, 1)):
+            response_tile(0, r, lh, SUM_TAG)
+            store(0, r, lh, on_scalar)
+        for r in range(ROW_TILES):
+            group_pattern(1, 1, on_vector, r, 1)
+        for r in range(ROW_TILES):
+            quantize_pattern(1, 1, r, 1)
+        copy_of = (on_scalar, on_vector)
         for lh in range(2):
-            response_pass(1, 0, lh, 0, "turn")
+            response_pass(1, 0, lh, 0, TURN_TAG)
         for lh in range(2):
-            response_pass(1, 0, lh, 1, "turn")
-            store(1, 0, lh, S if lh == 0 else V)
+            response_pass(1, 0, lh, 1, TURN_TAG)
+            store(1, 0, lh, copy_of[lh])
         for lh in range(2):
-            for s in range(G2):
-                response_pass(1, 1, lh, s, "turn")
-            store(1, 1, lh, S if lh == 0 else V)
+            response_tile(1, 1, lh, TURN_TAG)
+            store(1, 1, lh, copy_of[lh])

from contextlib import ExitStack

import concourse.mybir as mybir
from concourse.masks import make_identity

A, M, K, N, L = 3, 512, 2048, 1024, 1024
FLOPS = 2 * A * M * K * N + 2 * M * N * L

F32 = mybir.dt.float32
BF16 = mybir.dt.bfloat16
I32 = mybir.dt.int32
U32 = mybir.dt.uint32
U8 = mybir.dt.uint8
E4M3 = mybir.dt.float8_e4m3fn_x4
E5M2 = mybir.dt.float8_e5m2_x4
E2M1 = mybir.dt.float4_e2m1fn_x4
MULT = mybir.AluOpType.mult
ADD = mybir.AluOpType.add
COPY = mybir.ActivationFunctionType.Copy

P = 128
SLOTS = 4
PASS = P * SLOTS
BANK = 512
I_PASSES = K // PASS
J_PASSES = N // PASS
HALF = M // 2
ROW_TILES = HALF // P
J_TILES = N // P
FORM_COLS = 8
GROUPS = [((0, 0), (1, 0)), ((2, 0), (0, 1)), ((1, 1), (2, 1))]
SUM_TAG, TURN_TAG = "debye", "turn"
PSUM_BUFS = 4
OPEN_TILES = PSUM_BUFS
SORTED_BUFS = 8
RESP_BUFS = J_PASSES * (L // BANK)


def tile_powder_pattern_debye_s9_kernel(tc, hist, basis_words, basis_scales, form, resp, out):
    nc = tc.nc
    with ExitStack() as ctx:
        keep = ctx.enter_context(tc.tile_pool(name="keep", bufs=1))
        stage = ctx.enter_context(tc.tile_pool(name="stage", bufs=3))
        psum = ctx.enter_context(tc.psum_pool(name="psum", bufs=PSUM_BUFS))
        ctx.enter_context(tc.manual_schedule())
        on_vector = nc.vector.tensor_copy
        on_scalar = nc.scalar.copy

        def kept(shape, dtype, name):
            return keep.tile(shape, dtype, name=name, align_bytes=64)

        scales_raw = []
        for s in range(J_PASSES):
            scales_raw.append(kept([P, I_PASSES * PASS], U8, "scales_raw_%d" % s))
            nc.vector.memset(scales_raw[s][:].bitcast(I32), 0)
        ident = kept([P, P], F32, "ident")
        make_identity(nc, ident[:])
        form_raw = kept([A * J_PASSES, PASS], BF16, "form_raw")
        nc.gpsimd.dma_start(out=form_raw[:], in_=form.rearrange("c (s j) -> (c s) j", s=J_PASSES))
        form_rows = kept([P, PASS], BF16, "form_rows")
        nc.vector.memset(form_rows[:], 0.0)
        ident_bf = kept([P, FORM_COLS], BF16, "ident_bf")
        nc.vector.tensor_copy(out=ident_bf[:], in_=ident[:, :FORM_COLS])

        hist_raw = {}
        basis_raw = {}
        resp_raw = []

        def load_hist(grp, g0, passes):
            for part, (c, h) in enumerate(GROUPS[grp]):
                raw = kept([P, ROW_TILES, passes * PASS], BF16, "hist_%d_%d_%d" % (grp, part, g0))
                rows = hist[c, h * HALF : (h + 1) * HALF, g0 * PASS : (g0 + passes) * PASS]
                nc.sync.dma_start(out=raw[:], in_=rows.rearrange("(r x) i -> x r i", r=ROW_TILES))
                for g in range(passes):
                    hist_raw[grp, part, g0 + g] = (raw, g)

        def load_basis(s, g0, passes):
            raw = kept([P, passes, 2 * PASS], U8, "basis_raw_%d_%d" % (s, g0))
            src = basis_words[g0 : g0 + passes, :, s * 2 * PASS : (s + 1) * 2 * PASS].bitcast(I32)
            nc.sync.dma_start(out=raw[:].bitcast(I32), in_=src.rearrange("g p w -> p g w"))
            for g in range(passes):
                basis_raw[s, g0 + g] = raw[:, g, :]

        def load_basis_scales(s, queue):
            src = basis_scales[:, :, s * PASS : (s + 1) * PASS].bitcast(I32).rearrange("g (u v) n -> v u g n", v=4)
            for v in range(4):
                queue.dma_start(
                    out=scales_raw[s][v:P:32, :].bitcast(I32).rearrange("u (g n) -> u g n", g=I_PASSES), in_=src[v]
                )

        def load_resp(s):
            raw = kept([P, SLOTS, L], BF16, "resp_raw_%d" % s)
            src = resp[s * PASS : (s + 1) * PASS, :].rearrange("(a t b) l -> b a t l", t=SLOTS, b=4)
            for b in range(4):
                nc.sync.dma_start(out=raw[b:P:4, :, :], in_=src[b])
            resp_raw.append(raw)

        for g in range(I_PASSES):
            load_hist(0, g, 1)
            load_basis(0, g, 1)
            if g == 0:
                load_basis_scales(0, nc.scalar)
        load_hist(1, 0, 1)
        load_basis_scales(1, nc.sync)
        load_basis(1, 0, I_PASSES)
        load_hist(1, 1, 1)
        load_hist(1, 2, 2)
        for s in range(J_PASSES):
            load_resp(s)
            load_hist(2, 2 * s, 2)

        basis_codes = {}
        basis_plane = {}

        def sort_basis(s, g):
            codes = kept([P, 2 * PASS], U8, "basis_codes_%d_%d" % (g, s))
            nc.vector.tensor_copy(
                out=codes[:].bitcast(I32).rearrange("p (t a w) -> p t a w", t=SLOTS, w=2),
                in_=basis_raw[s, g].bitcast(I32).rearrange("p (a t w) -> p t a w", t=SLOTS, w=2),
            )
            basis_codes[s, g] = codes

        def sort_basis_scales(s):
            plane = kept([P, I_PASSES, PASS], U8, "basis_plane_%d" % s)
            nc.vector.tensor_copy(
                out=plane[:].bitcast(I32).rearrange("p g (t a) -> p g t a", t=SLOTS),
                in_=scales_raw[s][:].bitcast(I32).rearrange("p (g a t) -> p g t a", g=I_PASSES, t=SLOTS),
            )
            basis_plane[s] = plane

        hist_sorted = {}
        turn_bank = {}
        hist_grouped = {}
        hist_codes = {}
        hist_plane = {}

        def sort_hist(grp, g, engine_copy):
            for part in range(2):
                raw, g_local = hist_raw[grp, part, g]
                words = raw[:].bitcast(F32)[:, :, g_local * 2 * P : (g_local + 1) * 2 * P]
                ordered = stage.tile([P, ROW_TILES, 2, P], F32, name="hist_sorted", bufs=SORTED_BUFS, align_bytes=64)
                engine_copy(
                    out=ordered[:].rearrange("x r u (y e) -> x r y u e", e=4),
                    in_=words.rearrange("x r (y e u) -> x r y u e", e=4, u=2),
                )
                hist_sorted[grp, g, part] = ordered

        def turn_hist(grp, g):
            for part in range(2):
                bank = psum.tile([P, ROW_TILES, 2, P], F32, name=TURN_TAG)
                turn_bank[grp, g, part] = bank
                for r in range(ROW_TILES):
                    for u in range(2):
                        if (grp, g, part) in hist_sorted:
                            src = hist_sorted[grp, g, part][:, r, u, :]
                        else:
                            raw, g_local = hist_raw[grp, part, g]
                            src = raw[:, r, g_local * PASS : (g_local + 1) * PASS].bitcast(F32)[:, u : 2 * P : 2]
                        nc.tensor.transpose(bank[:, r, u, :], src, ident[:])

        def group_hist(grp, g):
            grouped = stage.tile([P, SLOTS * BANK], BF16, name="hist_grouped", align_bytes=64)
            hist_grouped[grp, g] = grouped
            for part in range(2):
                dst = grouped[:, part * SLOTS * HALF : (part + 1) * SLOTS * HALF].bitcast(F32)
                nc.scalar.copy(
                    out=dst.rearrange("p (r x u) -> p r x u", r=ROW_TILES, u=2),
                    in_=turn_bank[grp, g, part][:].rearrange("p r u x -> p r x u"),
                )

        def quantize_hist(grp, g):
            codes = kept([P, BANK], U32, "hist_codes_%d_%d" % (grp, g))
            plane = kept([P, BANK], U8, "hist_plane_%d_%d" % (grp, g))
            nc.vector.quantize_mx(out=codes[:].bitcast(E4M3), scales=plane[:], in_=hist_grouped[grp, g][:])
            hist_codes[grp, g] = codes
            hist_plane[grp, g] = plane

        debye_bank = {}

        def debye_pass(grp, tile, g, tag=SUM_TAG):
            s, t = divmod(tile, SLOTS)
            if g == 0:
                debye_bank[grp, tile] = psum.tile([P, BANK], F32, name=tag)
            nc.tensor.matmul_mx(
                out=debye_bank[grp, tile][:],
                lhsT=basis_codes[s, g][:, 2 * P * t : 2 * P * (t + 1)].bitcast(E2M1),
                lhsT_scale=basis_plane[s][:, g, P * t : P * (t + 1)],
                rhs=hist_codes[grp, g][:].bitcast(E4M3),
                rhs_scale=hist_plane[grp, g][:],
                start=(g == 0),
                stop=(g == I_PASSES - 1),
            )

        def debye_step(grp, g):
            for tile in range(OPEN_TILES):
                debye_pass(grp, tile, g)

        def debye_tile(grp, tile, tag=SUM_TAG):
            for g in range(I_PASSES):
                debye_pass(grp, tile, g, tag)

        form_cols = kept([P, SLOTS, FORM_COLS], F32, "form_cols")

        def sort_form():
            nc.scalar.copy(
                out=form_rows[: A * J_PASSES, :].rearrange("n (t a b) -> n t a b", t=SLOTS, b=4),
                in_=form_raw[:].rearrange("n (a t b) -> n t a b", t=SLOTS, b=4),
            )

        def spread_form():
            bank = psum.tile([P, SLOTS, FORM_COLS], F32, name=TURN_TAG)
            for t in range(SLOTS):
                nc.tensor.matmul(
                    bank[:, t, :], lhsT=form_rows[:, t * P : (t + 1) * P], rhs=ident_bf[:], start=True, stop=True
                )
            nc.scalar.copy(out=form_cols[:], in_=bank[:])

        partial = {}
        pattern = {}
        for h in range(2):
            for s in range(J_PASSES):
                pattern[h, s] = kept([P, SLOTS, HALF], BF16, "pattern_%d_%d" % (h, s))

        def weigh(grp, tile, part, lo=0, hi=HALF):
            c, h = GROUPS[grp][part]
            s, t = divmod(tile, SLOTS)
            src = debye_bank[grp, tile][:, part * HALF + lo : part * HALF + hi]
            row = c * J_PASSES + s
            weight = form_cols[:, t, row : row + 1]
            if c == 0:
                partial[h, tile] = kept([P, HALF], F32, "partial_%d_%d" % (h, tile))
                nc.scalar.activation(out=partial[h, tile][:], in_=src, func=COPY, scale=weight)
            else:
                dst = pattern[h, s][:, t, lo:hi] if c == A - 1 else partial[h, tile][:, lo:hi]
                nc.vector.scalar_tensor_tensor(
                    out=dst, in0=src, scalar=weight, in1=partial[h, tile][:, lo:hi], op0=MULT, op1=ADD
                )

        def weigh_both(grp, tile):
            weigh(grp, tile, 0)
            weigh(grp, tile, 1)

        def interleave(engine_copy, dst, src):
            engine_copy(
                out=dst.rearrange("p (y e t) -> p y t e", e=4, t=SLOTS),
                in_=src.rearrange("p t (y e) -> p y t e", e=4),
            )

        resp_grouped = {}
        resp_codes = {}
        resp_plane = {}

        def group_resp(s, lh, engine_copy, lo=0, hi=BANK):
            if lo == 0:
                resp_grouped[s, lh] = stage.tile(
                    [P, SLOTS * BANK], BF16, name="resp_grouped", bufs=RESP_BUFS, align_bytes=64
                )
            src = resp_raw[s][:, :, lh * BANK + lo : lh * BANK + hi]
            interleave(engine_copy, resp_grouped[s, lh][:, SLOTS * lo : SLOTS * hi], src)

        def quantize_resp(s, lh):
            codes = kept([P, BANK], U32, "resp_codes_%d_%d" % (s, lh))
            plane = kept([P, BANK], U8, "resp_plane_%d_%d" % (s, lh))
            nc.vector.quantize_mx(out=codes[:].bitcast(E4M3), scales=plane[:], in_=resp_grouped[s, lh][:])
            resp_codes[s, lh] = codes
            resp_plane[s, lh] = plane

        pattern_grouped = {}
        pattern_codes = {}
        pattern_plane = {}

        def group_pattern(h, s, engine_copy, r0=0, count=ROW_TILES):
            grouped = kept([P, SLOTS * P * count], BF16, "pattern_grouped_%d_%d_%d" % (h, s, r0))
            interleave(engine_copy, grouped[:], pattern[h, s][:, :, r0 * P : (r0 + count) * P])
            pattern_grouped[h, s, r0] = grouped

        def quantize_pattern(h, s, r0=0, count=ROW_TILES):
            codes = kept([P, P * count], U32, "pattern_codes_%d_%d_%d" % (h, s, r0))
            plane = kept([P, P * count], U8, "pattern_plane_%d_%d_%d" % (h, s, r0))
            nc.vector.quantize_mx(out=codes[:].bitcast(E5M2), scales=plane[:], in_=pattern_grouped[h, s, r0][:])
            for r in range(count):
                pattern_codes[h, s, r0 + r] = codes[:, r * P : (r + 1) * P]
                pattern_plane[h, s, r0 + r] = plane[:, r * P : (r + 1) * P]

        out_bank = {}

        def response_pass(h, r, lh, s, tag):
            if s == 0:
                out_bank[h, r, lh] = psum.tile([P, BANK], F32, name=tag)
            nc.tensor.matmul_mx(
                out=out_bank[h, r, lh][:],
                lhsT=pattern_codes[h, s, r].bitcast(E5M2),
                lhsT_scale=pattern_plane[h, s, r],
                rhs=resp_codes[s, lh][:].bitcast(E4M3),
                rhs_scale=resp_plane[s, lh][:],
                start=(s == 0),
                stop=(s == J_PASSES - 1),
            )

        def response_tile(h, r, lh, tag):
            for s in range(J_PASSES):
                response_pass(h, r, lh, s, tag)

        def store(h, r, lh, engine_copy):
            result = kept([P, BANK], F32, "result_%d_%d_%d" % (h, r, lh))
            engine_copy(out=result[:], in_=out_bank[h, r, lh][:])
            m0 = h * HALF + r * P
            nc.sync.dma_start(out=out[m0 : m0 + P, lh * BANK : (lh + 1) * BANK], in_=result[:])

        turn_hist(0, 0)
        sort_basis(0, 0)
        sort_basis_scales(0)
        group_hist(0, 0)
        quantize_hist(0, 0)
        for g in range(1, I_PASSES):
            turn_hist(0, g)
            group_hist(0, g)
            sort_basis(0, g)
            if g == 1:
                sort_form()
            if g == I_PASSES - 1:
                spread_form()
            ahead_grp, ahead_g = divmod(g + 1, I_PASSES)
            sort_hist(ahead_grp, ahead_g, on_vector)
            quantize_hist(0, g)
            debye_step(0, g - 1)
        turn_hist(1, 0)
        group_hist(1, 0)
        debye_step(0, I_PASSES - 1)
        sort_basis_scales(1)
        for g in range(I_PASSES):
            sort_basis(1, g)
        debye_tile(0, 4, TURN_TAG)
        sort_hist(1, 1, on_vector)
        weigh_both(0, 0)
        quantize_hist(1, 0)
        for tile in range(1, OPEN_TILES):
            weigh_both(0, tile)
        debye_tile(0, 5)
        weigh_both(0, 4)
        turn_hist(1, 1)
        weigh_both(0, 5)
        group_hist(1, 1)
        sort_hist(1, 2, on_vector)
        debye_tile(0, 6)
        quantize_hist(1, 1)
        sort_hist(1, 3, on_vector)
        weigh_both(0, 6)
        debye_tile(0, 7)
        weigh_both(0, 7)

        for g in (2, 3):
            turn_hist(1, g)
        for g in (2, 3):
            group_hist(1, g)
        group_resp(0, 0, on_vector)
        for g in (2, 3):
            quantize_hist(1, g)
        sort_hist(2, 0, on_scalar)
        group_resp(0, 1, on_vector)
        group_resp(1, 0, on_scalar, 0, BANK // 2)
        for g in range(I_PASSES):
            debye_step(1, g)
        debye_tile(1, 4, TURN_TAG)
        for tile in range(OPEN_TILES):
            weigh_both(1, tile)
        sort_hist(2, 1, on_vector)
        weigh_both(1, 4)
        group_resp(1, 0, on_scalar, BANK // 2, BANK)
        debye_tile(1, 5)
        for g in (0, 1):
            turn_hist(2, g)
        group_pattern(0, 0, on_vector)
        weigh_both(1, 5)
        for g in (0, 1):
            group_hist(2, g)
        sort_hist(2, 2, on_vector)
        quantize_resp(0, 0)
        sort_hist(2, 3, on_vector)
        debye_tile(1, 6)
        quantize_hist(2, 0)
        weigh_both(1, 6)
        quantize_resp(1, 0)
        debye_tile(1, 7)
        quantize_hist(2, 1)
        weigh(1, 7, 1)
        weigh(1, 7, 0)

        for g in (2, 3):
            turn_hist(2, g)
        for g in (2, 3):
            group_hist(2, g)
        quantize_resp(0, 1)
        quantize_hist(2, 2)
        quantize_pattern(0, 0)
        quantize_hist(2, 3)
        group_pattern(0, 1, on_scalar)
        group_resp(1, 1, on_scalar)
        quantize_pattern(0, 1)
        for g in range(I_PASSES):
            debye_step(2, g)
        response_tile(0, 0, 0, TURN_TAG)
        debye_tile(2, 4, TURN_TAG)
        weigh(2, 0, 0)
        for tile in range(1, OPEN_TILES + 1):
            weigh(2, tile, 0)
            weigh(2, tile - 1, 1)
        store(0, 0, 0, on_scalar)
        group_pattern(1, 0, on_scalar)
        quantize_resp(1, 1)
        weigh(2, 4, 1)
        debye_tile(2, 5)
        weigh_both(2, 5)
        debye_tile(2, 6)
        weigh(2, 6, 0)
        quantize_pattern(1, 0)
        weigh(2, 6, 1)
        debye_tile(2, 7)

        for part in range(2):
            for r in range(ROW_TILES):
                weigh(2, J_TILES - 1, part, r * P, (r + 1) * P)
        for r, lh in ((0, 1), (1, 0), (1, 1)):
            response_tile(0, r, lh, SUM_TAG)
            store(0, r, lh, on_scalar)
        for r in range(ROW_TILES):
            group_pattern(1, 1, on_vector, r, 1)
        for r in range(ROW_TILES):
            quantize_pattern(1, 1, r, 1)
        copy_of = (on_scalar, on_vector)
        for lh in range(2):
            response_pass(1, 0, lh, 0, TURN_TAG)
        for lh in range(2):
            response_pass(1, 0, lh, 1, TURN_TAG)
            store(1, 0, lh, copy_of[lh])
        for lh in range(2):
            response_tile(1, 1, lh, TURN_TAG)
            store(1, 1, lh, copy_of[lh])
